import numpy as np
import ml_dtypes


def mxq(x, axis, fmt="e4m3"):
    dtype, down = {"e4m3": (ml_dtypes.float8_e4m3fn, 7), "e5m2": (ml_dtypes.float8_e5m2, 14)}[fmt]
    v = np.moveaxis(np.asarray(x, np.float32).astype(ml_dtypes.bfloat16).astype(np.float64), axis, -1)
    blocks = v.reshape(v.shape[:-1] + (-1, 32))
    amax = np.abs(blocks).max(-1, keepdims=True)
    byte = np.maximum(np.where(amax > 0, np.frexp(amax)[1] - 1 + 127, 0) - down, 1)
    scale = np.exp2(byte - 127.0)
    codes = (blocks / scale).astype(np.float32).astype(dtype).astype(np.float64)
    return np.moveaxis((codes * scale).reshape(v.shape), -1, axis)


WIDE = False


def mx_kscale(k):
    if not WIDE:
        return np.ones(k)
    levels = np.array([10, -10, 5, -5, 0])
    if k % 512:
        return np.exp2(np.random.permutation(np.resize(levels, k // 32))).repeat(32)
    a = np.empty((k // 512, 16))
    for p in range(k // 512):
        a[p, :8] = np.random.permutation(np.resize(levels, 8))
        for g in range(8):
            far = levels[np.abs(levels - a[p, g]) >= 10]
            a[p, g + 8] = far[np.random.randint(len(far))]
    return np.exp2(a.ravel()).repeat(32)


def f64(x):
    return np.asarray(x).astype(np.float64)


def striped(idx):
    return np.tile(idx.reshape(-1, 16).T, (8, 1)).astype(np.uint16)


def unstriped(offs):
    return offs[:16].T.reshape(-1).astype(np.int64)


def striped8(idx):
    return np.concatenate([x.reshape(-1, 16).T for x in idx]).astype(np.uint16)


def runs(offs, k):
    lists = np.stack([offs[16 * r : 16 * r + 16].T.reshape(-1) for r in range(8)]).astype(np.int64)
    return lists[np.arange(k) % 512 // 64]


def pack_weight(w):
    k, n = w.shape
    w = f64(np.asarray(w, np.float32).astype(ml_dtypes.bfloat16)).reshape(k // 32, 32, n)
    amax = np.abs(w).max(1)
    byte = np.clip(np.where(amax > 0, np.frexp(amax)[1] - 1 + 127 - 7, 1), 1, 254)
    scaled = (w * np.exp2(127.0 - byte)[:, None, :]).reshape(k, n).astype(np.float32)
    words = np.ascontiguousarray(scaled.reshape(k // 512, 128, 4, n).transpose(0, 1, 3, 2)).astype(ml_dtypes.float8_e4m3fn).view(np.uint8)
    return words, np.ascontiguousarray(byte.astype(np.uint8).reshape(k // 512, 16, n))


def unpack_weight(words, scales):
    g, p, n, _ = words.shape
    vals = np.ascontiguousarray(words).view(ml_dtypes.float8_e4m3fn).astype(np.float64) * np.repeat(np.exp2(scales.astype(np.float64) - 127.0), 8, axis=1)[..., None]
    return vals.transpose(0, 1, 3, 2).reshape(g * 512, n)


def relu(v):
    return np.maximum(v, 0.0)


K, T, S, N, H, U = 512, 2048, 512, 512, 512, 1024


def setup_inputs():
    n = np.random.standard_normal
    s = mx_kscale(K)[:, None]
    u = mx_kscale(H)
    packed_xT = pack_weight(n((K, T)) * s)
    return {
        "x_words": packed_xT[0],
        "x_scales": packed_xT[1],
        "w1": (n((K, H)) / np.sqrt(K) / s).astype(np.float32),
        "gamma": (np.random.uniform(0.5, 1.5, (H, U)) * u[:, None]).astype(np.float32),
        "beta": (n((H, U)) * u[:, None]).astype(np.float32),
        "w2": (n((H, N)) / np.sqrt(H) / u[:, None]).astype(np.float32),
        "offs": striped(np.random.permutation(T)[:S]),
        "sty": striped8(np.random.randint(0, U, (8, S))),
    }


def reference(x_words, x_scales, w1, gamma, beta, w2, offs, sty):
    xq = unpack_weight(x_words, x_scales)[:, unstriped(offs)]
    y = mxq(f64(w1), 0, "e4m3").T @ xq
    h = (y - y.mean(axis=1, keepdims=True)) / np.sqrt(y.var(axis=1, keepdims=True) + 1e-5)
    z = relu(h * (f64(gamma)[np.arange(H)[:, None], runs(sty, H)]) + f64(beta)[np.arange(H)[:, None], runs(sty, H)])
    return mxq(f64(w2), 0, "e4m3").T @ mxq(z, 0, "e4m3")

@@ -1,0 +1,204 @@
+from contextlib import ExitStack
+
+import concourse.mybir as mybir
+
+K, T, S, N, H, U = 512, 2048, 512, 512, 512, 1024
+FLOPS = 2 * K * H * S + 2 * H * N * S
+
+F32 = mybir.dt.float32
+BF16 = mybir.dt.bfloat16
+I32 = mybir.dt.int32
+U32 = mybir.dt.uint32
+U16 = mybir.dt.uint16
+U8 = mybir.dt.uint8
+FP8X4 = mybir.dt.float8_e4m3fn_x4
+ACT = mybir.ActivationFunctionType
+ALU = mybir.AluOpType
+
+P = 128
+PACK = 4
+HALF = S // 2
+EPS = 1e-5
+VECTOR_STATS = 3
+
+
+def tile_picked_adain8_relu_p_kernel(tc, x_words, x_scales, w1, gamma, beta, w2, offs, sty, out):
+    nc = tc.nc
+    with ExitStack() as ctx:
+        keep = ctx.enter_context(tc.tile_pool(name="keep", bufs=1))
+        psum = ctx.enter_context(tc.psum_pool(name="psum", bufs=1))
+
+        offs_sb = keep.tile([P, S // 16], U16, name="offs_sb")
+        sty_sb = keep.tile([P, S // 16], U16, name="sty_sb")
+        word_table = keep.tile([P, T], U32, name="word_table", align_bytes=64)
+        scale_table = keep.tile([P, T], U8, name="scale_table", align_bytes=64)
+        w1_raw = keep.tile([P, PACK, H], F32, name="w1_raw", align_bytes=64)
+        w2_raw = keep.tile([P, PACK, N], F32, name="w2_raw", tag="w2_then_z", align_bytes=64)
+        gamma_sb = [keep.tile([P, U], F32, name="gamma_%d" % t, align_bytes=64) for t in range(PACK)]
+        beta_sb = [keep.tile([P, U], F32, name="beta_%d" % t, align_bytes=64) for t in range(PACK)]
+        gamma_rows = gamma.rearrange("(p t) u -> p t u", t=PACK)
+        beta_rows = beta.rearrange("(p t) u -> p t u", t=PACK)
+
+        nc.vector.memset(scale_table[:].bitcast(I32), 0)
+        warm = keep.tile([P, 2], F32, name="warm")
+        nc.vector.memset(warm[:, 0:1], 1.0)
+        nc.scalar.activation(warm[:, 1:2], warm[:, 0:1], ACT.Abs_reciprocal_sqrt)
+        nc.sync.dma_start(w1_raw[:], w1.rearrange("(p j) c -> p j c", j=PACK))
+        for r in range(4):
+            nc.sync.dma_start(scale_table[r:P:32, :].bitcast(I32), x_scales[0, r:16:4, :].bitcast(I32))
+        nc.sync.dma_start(offs_sb[:], offs)
+        nc.sync.dma_start(word_table[:].bitcast(I32), x_words[0].rearrange("p n t -> p (n t)").bitcast(I32))
+        nc.sync.dma_start(sty_sb[:], sty)
+        for t in range(2):
+            nc.sync.dma_start(gamma_sb[t][:], gamma_rows[:, t, :])
+            nc.sync.dma_start(beta_sb[t][:], beta_rows[:, t, :])
+        nc.sync.dma_start(w2_raw[:], w2.rearrange("(p j) c -> p j c", j=PACK))
+        for t in range(2, PACK):
+            nc.sync.dma_start(gamma_sb[t][:], gamma_rows[:, t, :])
+        for t in range(2, PACK):
+            nc.sync.dma_start(beta_sb[t][:], beta_rows[:, t, :])
+
+        x_scale = keep.tile([P, S], U8, name="x_scale", align_bytes=64)
+        nc.vector.tensor_copy(x_scale[:], scale_table[:].indirect(offs_sb[:]))
+
+        w1_codes, w1_scale = [], []
+        for u in range(2):
+            grouped = keep.tile([P, 2 * P * PACK], BF16, name="w1_bf16_%d" % u, align_bytes=64)
+            dst = grouped[:].rearrange("p (t m j) -> p m t j", t=2, j=PACK)
+            src = w1_raw[:].rearrange("p j (m t) -> p m t j", t=PACK)[:, :, 2 * u : 2 * u + 2, :]
+            if u == 0:
+                nc.vector.tensor_copy(dst, src)
+            else:
+                nc.scalar.copy(dst, src)
+            codes = keep.tile([P, 2 * P], U32, name="w1_codes_%d" % u, align_bytes=64)
+            scale = keep.tile([P, 2 * P], U8, name="w1_scale_%d" % u, align_bytes=64)
+            nc.vector.quantize_mx(out=codes[:].bitcast(FP8X4), scales=scale[:], in_=grouped[:])
+            w1_codes.append(codes)
+            w1_scale.append(scale)
+
+        x_codes = keep.tile([P, S], U32, name="x_codes", align_bytes=64)
+        nc.vector.tensor_copy(x_codes[:], word_table[:].indirect(offs_sb[:]))
+
+        y = []
+        for t in range(PACK):
+            bank = psum.tile([P, S], F32, name="y_%d" % t, tag="y_%d" % t)
+            cols = slice((t % 2) * P, (t % 2 + 1) * P)
+            nc.tensor.matmul_mx(
+                out=bank[:],
+                lhsT=w1_codes[t // 2][:, cols].bitcast(FP8X4),
+                lhsT_scale=w1_scale[t // 2][:, cols],
+                rhs=x_codes[:].bitcast(FP8X4),
+                rhs_scale=x_scale[:],
+                start=True,
+                stop=True,
+            )
+            y.append(bank)
+
+        h = [keep.tile([P, S], F32, name="h_%d" % t, align_bytes=64) for t in range(PACK)]
+
+        def normalise(t):
+            small = keep.tile([P, 8], F32, name="small_%d" % t, tag="small_%d" % (t % 2))
+            neg_mean, sum_sq, rstd, shift = small[:, 0:1], small[:, 1:2], small[:, 2:3], small[:, 3:4]
+            if t < VECTOR_STATS:
+                stats = keep.tile([P, 8], F32, name="stats_%d" % t)
+                nc.vector.bn_stats(stats[:, 0:6], y[t][:])
+                nc.vector.bn_aggr(stats[:, 6:8], stats[:, 0:6])
+                nc.scalar.activation(rstd, stats[:, 7:8], ACT.Abs_reciprocal_sqrt, bias=EPS)
+                nc.scalar.activation(neg_mean, stats[:, 6:7], ACT.Copy, scale=-1.0)
+            else:
+                nc.scalar.activation(h[t][:], y[t][:], ACT.Copy, scale=-1.0 / S, accum_out=neg_mean)
+                nc.scalar.activation(h[t][:], y[t][:], ACT.Square, bias=neg_mean, accum_out=sum_sq)
+                nc.scalar.activation(rstd, sum_sq, ACT.Abs_reciprocal_sqrt, scale=1.0 / S, bias=EPS)
+            nc.scalar.activation(shift, rstd, ACT.Copy, scale=neg_mean)
+            nc.scalar.activation(h[t][:], y[t][:], ACT.Identity, scale=rstd, bias=shift)
+
+        scaled = {(t, a): keep.tile([P, HALF], F32, name="scaled_%d_%d" % (t, a), tag="scaled_%d_%d" % (t, a), align_bytes=64)[:] for t in range(PACK) for a in range(2) if (t, a) != (3, 1)}
+        pre = {(u, a): keep.tile([P, 2, HALF], F32, name="pre_%d_%d" % (u, a), align_bytes=64)[:] for u in range(2) for a in range(2) if (u, a) != (1, 1)}
+
+        def styles(a):
+            return sty_sb[:, a * HALF // 16 : (a + 1) * HALF // 16]
+
+        def scale_by_gamma(t, a):
+            nc.vector.tensor_tensor(scaled[t, a], gamma_sb[t][:].indirect(styles(a)), h[t][:, a * HALF : (a + 1) * HALF], ALU.mult)
+
+        def shift_by_beta(t, a):
+            nc.vector.tensor_tensor(pre[t // 2, a][:, t % 2, :], beta_sb[t][:].indirect(styles(a)), scaled[t, a], ALU.add)
+
+        def rectify(u, a, on_vector):
+            dst = z_bf16[a].rearrange("p (s t) -> p s t", t=PACK)[:, :, 2 * u : 2 * u + 2]
+            src = pre[u, a].rearrange("p e s -> p s e")
+            if on_vector:
+                nc.vector.tensor_scalar(dst, src, 0.0, None, ALU.max)
+            else:
+                nc.scalar.activation(dst, src, ACT.Relu)
+
+        w2_bf16 = keep.tile([P, N * PACK], BF16, name="w2_bf16", align_bytes=64)
+        w2_codes = keep.tile([P, N], U32, name="w2_codes", align_bytes=64)
+        w2_scale = keep.tile([P, N], U8, name="w2_scale", align_bytes=64)
+
+        def cast_w2(g):
+            cols = slice(g * N // 2, (g + 1) * N // 2)
+            dst = w2_bf16[:].rearrange("p (c j) -> p c j", j=PACK)[:, cols, :].rearrange("p (c i) j -> p c j i", i=4)
+            src = w2_raw[:, :, cols].rearrange("p j (c i) -> p c j i", i=4)
+            nc.scalar.copy(dst, src)
+
+        z_codes = [keep.tile([P, HALF], U32, name="z_codes_%d" % a, align_bytes=64) for a in range(2)]
+        z_scale = [keep.tile([P, HALF], U8, name="z_scale_%d" % a, align_bytes=64) for a in range(2)]
+
+        def quantise_z(a):
+            nc.vector.quantize_mx(out=z_codes[a][:].bitcast(FP8X4), scales=z_scale[a][:], in_=z_bf16[a])
+
+        def project(a, first, count, bank_tag, on_vector):
+            bank = psum.tile([P, count, HALF], F32, name="o_%d_%d" % (a, first), tag=bank_tag)
+            for e in range(count):
+                cols = slice((first + e) * P, (first + e + 1) * P)
+                nc.tensor.matmul_mx(
+                    out=bank[:, e, :],
+                    lhsT=w2_codes[:, cols].bitcast(FP8X4),
+                    lhsT_scale=w2_scale[:, cols],
+                    rhs=z_codes[a][:].bitcast(FP8X4),
+                    rhs_scale=z_scale[a][:],
+                    start=True,
+                    stop=True,
+                )
+            staged = keep.tile([P, count, HALF], F32, name="staged_%d_%d" % (a, first), align_bytes=64)
+            if on_vector:
+                nc.vector.tensor_copy(staged[:], bank[:])
+            else:
+                nc.scalar.copy(staged[:], bank[:])
+            rows = out[first * P : (first + count) * P, a * HALF : (a + 1) * HALF]
+            nc.sync.dma_start(rows.rearrange("(e p) n -> p e n", p=P), staged[:])
+
+        for t in range(PACK):
+            normalise(t)
+        for t in range(2):
+            for a in range(2):
+                scale_by_gamma(t, a)
+            for a in range(2):
+                shift_by_beta(t, a)
+        for g in range(2):
+            cast_w2(g)
+        z_all = keep.tile([P, S * PACK], BF16, name="z_all", tag="w2_then_z", align_bytes=64)
+        z_bf16 = [z_all[:, a * HALF * PACK : (a + 1) * HALF * PACK] for a in range(2)]
+        for a in range(2):
+            rectify(0, a, False)
+        scale_by_gamma(2, 0)
+        scale_by_gamma(2, 1)
+        scale_by_gamma(3, 0)
+        nc.vector.quantize_mx(out=w2_codes[:].bitcast(FP8X4), scales=w2_scale[:], in_=w2_bf16[:])
+        shift_by_beta(2, 0)
+        shift_by_beta(3, 0)
+        rectify(1, 0, False)
+        last = keep.tile([P, 3, HALF], F32, name="last", tag="scaled_3_0", align_bytes=64)
+        scaled[3, 1] = last[:, 0, :]
+        pre[1, 1] = last[:, 1:3, :]
+        scale_by_gamma(3, 1)
+        shift_by_beta(2, 1)
+        shift_by_beta(3, 1)
+        quantise_z(0)
+        rectify(1, 1, True)
+        project(0, 0, 2, "out_0", False)
+        quantise_z(1)
+        project(0, 2, 2, "out_1", True)
+        for m in range(PACK):
+            project(1, m, 1, "y_%d" % m, m % 2 == 0)

@@ -19,7 +19,8 @@ P = 128
 PACK = 4
 HALF = S // 2
 EPS = 1e-5
-VECTOR_STATS = 3
+EARLY = 2
+QUARTER = S // 4
 
 
 def tile_picked_adain8_relu_p_kernel(tc, x_words, x_scales, w1, gamma, beta, w2, offs, sty, out):
@@ -33,7 +34,7 @@ def tile_picked_adain8_relu_p_kernel(tc, x_words, x_scales, w1, gamma, beta, w2,
         word_table = keep.tile([P, T], U32, name="word_table", align_bytes=64)
         scale_table = keep.tile([P, T], U8, name="scale_table", align_bytes=64)
         w1_raw = keep.tile([P, PACK, H], F32, name="w1_raw", align_bytes=64)
-        w2_raw = keep.tile([P, PACK, N], F32, name="w2_raw", tag="w2_then_z", align_bytes=64)
+        w2_raw = keep.tile([P, PACK, N], F32, name="w2_raw", align_bytes=64)
         gamma_sb = [keep.tile([P, U], F32, name="gamma_%d" % t, align_bytes=64) for t in range(PACK)]
         beta_sb = [keep.tile([P, U], F32, name="beta_%d" % t, align_bytes=64) for t in range(PACK)]
         gamma_rows = gamma.rearrange("(p t) u -> p t u", t=PACK)
@@ -49,14 +50,14 @@ def tile_picked_adain8_relu_p_kernel(tc, x_words, x_scales, w1, gamma, beta, w2,
         nc.sync.dma_start(offs_sb[:], offs)
         nc.sync.dma_start(word_table[:].bitcast(I32), x_words[0].rearrange("p n t -> p (n t)").bitcast(I32))
         nc.sync.dma_start(sty_sb[:], sty)
-        for t in range(2):
-            nc.sync.dma_start(gamma_sb[t][:], gamma_rows[:, t, :])
+        for t in range(EARLY):
             nc.sync.dma_start(beta_sb[t][:], beta_rows[:, t, :])
+            nc.sync.dma_start(gamma_sb[t][:], gamma_rows[:, t, :])
+        nc.sync.dma_start(gamma_sb[2][:], gamma_rows[:, 2, :])
+        nc.sync.dma_start(beta_sb[2][:], beta_rows[:, 2, :])
         nc.sync.dma_start(w2_raw[:], w2.rearrange("(p j) c -> p j c", j=PACK))
-        for t in range(2, PACK):
-            nc.sync.dma_start(gamma_sb[t][:], gamma_rows[:, t, :])
-        for t in range(2, PACK):
-            nc.sync.dma_start(beta_sb[t][:], beta_rows[:, t, :])
+        nc.sync.dma_start(gamma_sb[3][:], gamma_rows[:, 3, :])
+        nc.sync.dma_start(beta_sb[3][:], beta_rows[:, 3, :])
 
         x_scale = keep.tile([P, S], U8, name="x_scale", align_bytes=64)
         nc.vector.tensor_copy(x_scale[:], scale_table[:].indirect(offs_sb[:]))
@@ -94,111 +95,126 @@ def tile_picked_adain8_relu_p_kernel(tc, x_words, x_scales, w1, gamma, beta, w2,
             )
             y.append(bank)
 
-        h = [keep.tile([P, S], F32, name="h_%d" % t, align_bytes=64) for t in range(PACK)]
+        unused = keep.tile([P, S], BF16, name="unused", align_bytes=64)
+        neg_mean, rstd = {}, {}
+        pre = [keep.tile([P, PACK, HALF], F32, name="pre_%d" % a, align_bytes=64) for a in range(2)]
+        h = {(t, a): keep.tile([P, HALF], F32, name="h_%d_%d" % (t, a), align_bytes=64)[:] for t, a in ((2, 0), (2, 1), (3, 1))}
+        h[3, 0] = pre[1][:, 2, :]
 
-        def normalise(t):
-            small = keep.tile([P, 8], F32, name="small_%d" % t, tag="small_%d" % (t % 2))
-            neg_mean, sum_sq, rstd, shift = small[:, 0:1], small[:, 1:2], small[:, 2:3], small[:, 3:4]
-            if t < VECTOR_STATS:
-                stats = keep.tile([P, 8], F32, name="stats_%d" % t)
-                nc.vector.bn_stats(stats[:, 0:6], y[t][:])
-                nc.vector.bn_aggr(stats[:, 6:8], stats[:, 0:6])
-                nc.scalar.activation(rstd, stats[:, 7:8], ACT.Abs_reciprocal_sqrt, bias=EPS)
-                nc.scalar.activation(neg_mean, stats[:, 6:7], ACT.Copy, scale=-1.0)
-            else:
-                nc.scalar.activation(h[t][:], y[t][:], ACT.Copy, scale=-1.0 / S, accum_out=neg_mean)
-                nc.scalar.activation(h[t][:], y[t][:], ACT.Square, bias=neg_mean, accum_out=sum_sq)
-                nc.scalar.activation(rstd, sum_sq, ACT.Abs_reciprocal_sqrt, scale=1.0 / S, bias=EPS)
-            nc.scalar.activation(shift, rstd, ACT.Copy, scale=neg_mean)
-            nc.scalar.activation(h[t][:], y[t][:], ACT.Identity, scale=rstd, bias=shift)
+        def half(a):
+            return slice(a * HALF, (a + 1) * HALF)
 
-        scaled = {(t, a): keep.tile([P, HALF], F32, name="scaled_%d_%d" % (t, a), tag="scaled_%d_%d" % (t, a), align_bytes=64)[:] for t in range(PACK) for a in range(2) if (t, a) != (3, 1)}
-        pre = {(u, a): keep.tile([P, 2, HALF], F32, name="pre_%d_%d" % (u, a), align_bytes=64)[:] for u in range(2) for a in range(2) if (u, a) != (1, 1)}
+        def statistics(t):
+            small = keep.tile([P, 4], F32, name="small_%d" % t, tag="small_%d" % min(t, EARLY), align_bytes=64)
+            neg_mean[t], sum_sq, rstd[t], shift = small[:, 0:1], small[:, 1:2], small[:, 2:3], small[:, 3:4]
+            nc.scalar.activation(unused[:], y[t][:], ACT.Copy, scale=-1.0 / S, accum_out=neg_mean[t])
+            nc.scalar.activation(unused[:], y[t][:], ACT.Square, bias=neg_mean[t], accum_out=sum_sq)
+            nc.scalar.activation(rstd[t], sum_sq, ACT.Abs_reciprocal_sqrt, scale=1.0 / S, bias=EPS)
+            if t >= EARLY:
+                nc.scalar.activation(shift, rstd[t], ACT.Copy, scale=neg_mean[t])
+                for a in range(2):
+                    nc.scalar.activation(h[t, a], y[t][:, half(a)], ACT.Identity, scale=rstd[t], bias=shift)
+
+        scaled = {}
 
         def styles(a):
             return sty_sb[:, a * HALF // 16 : (a + 1) * HALF // 16]
 
-        def scale_by_gamma(t, a):
-            nc.vector.tensor_tensor(scaled[t, a], gamma_sb[t][:].indirect(styles(a)), h[t][:, a * HALF : (a + 1) * HALF], ALU.mult)
+        def modulate_early(t):
+            picked_beta = keep.tile([P, S], F32, name="picked_beta_%d" % t, align_bytes=64)
+            nc.vector.tensor_copy(picked_beta[:], beta_sb[t][:].indirect(sty_sb[:]))
+            picked_gamma = [keep.tile([P, HALF], F32, name="picked_gamma_%d_%d" % (t, a), align_bytes=64) for a in range(2)]
+            for a in range(2):
+                nc.vector.tensor_copy(picked_gamma[a][:], gamma_sb[t][:].indirect(styles(a)))
+            for a in range(2):
+                scaled[t, a] = keep.tile([P, HALF], F32, name="scaled_%d_%d" % (t, a), align_bytes=64)
+                nc.vector.scalar_tensor_tensor(scaled[t, a][:], y[t][:, half(a)], neg_mean[t], picked_gamma[a][:], ALU.add, ALU.mult)
+            for a in range(2):
+                nc.vector.scalar_tensor_tensor(pre[a][:, t, :], scaled[t, a][:], rstd[t], picked_beta[:, half(a)], ALU.mult, ALU.add)
 
-        def shift_by_beta(t, a):
-            nc.vector.tensor_tensor(pre[t // 2, a][:, t % 2, :], beta_sb[t][:].indirect(styles(a)), scaled[t, a], ALU.add)
+        def scale_late(t, a):
+            scaled[t, a] = keep.tile([P, HALF], F32, name="scaled_%d_%d" % (t, a), tag="scaled_3" if t == 3 else "scaled_2_%d" % a, align_bytes=64)
+            nc.vector.tensor_tensor(scaled[t, a][:], gamma_sb[t][:].indirect(styles(a)), h[t, a], ALU.mult)
 
-        def rectify(u, a, on_vector):
-            dst = z_bf16[a].rearrange("p (s t) -> p s t", t=PACK)[:, :, 2 * u : 2 * u + 2]
-            src = pre[u, a].rearrange("p e s -> p s e")
+        def shift_late(t, a):
+            nc.vector.tensor_tensor(pre[a][:, t, :], beta_sb[t][:].indirect(styles(a)), scaled[t, a][:], ALU.add)
+
+        w2_codes, w2_scale = [], []
+
+        def quantise_w2(g):
+            grouped = w2_bf16[:, g * 2 * P * PACK : (g + 1) * 2 * P * PACK]
+            dst = grouped.rearrange("p (c i j) -> p c j i", i=4, j=PACK)
+            src = w2_raw[:, :, 2 * g * P : 2 * (g + 1) * P].rearrange("p j (c i) -> p c j i", i=4)
+            nc.scalar.copy(dst, src)
+            codes = keep.tile([P, 2 * P], U32, name="w2_codes_%d" % g, align_bytes=64)
+            scale = keep.tile([P, 2 * P], U8, name="w2_scale_%d" % g, align_bytes=64)
+            nc.vector.quantize_mx(out=codes[:].bitcast(FP8X4), scales=scale[:], in_=grouped)
+            w2_codes.append(codes)
+            w2_scale.append(scale)
+
+        z_bf16 = [pre[1][:, 3, :].bitcast(BF16)]
+        z_bf16.extend(keep.tile([P, QUARTER * PACK], BF16, name="z_bf16_%d" % q, align_bytes=64)[:] for q in range(1, 4))
+        z_codes = [keep.tile([P, QUARTER], U32, name="z_codes_%d" % q, align_bytes=64) for q in range(4)]
+        z_scale = [keep.tile([P, QUARTER], U8, name="z_scale_%d" % q, align_bytes=64) for q in range(4)]
+
+        def rectify(q, on_vector):
+            dst = z_bf16[q].rearrange("p (c i t) -> p c t i", i=4, t=PACK)
+            src = pre[q // 2][:, :, (q % 2) * QUARTER : (q % 2 + 1) * QUARTER].rearrange("p t (c i) -> p c t i", i=4)
             if on_vector:
                 nc.vector.tensor_scalar(dst, src, 0.0, None, ALU.max)
             else:
                 nc.scalar.activation(dst, src, ACT.Relu)
 
-        w2_bf16 = keep.tile([P, N * PACK], BF16, name="w2_bf16", align_bytes=64)
-        w2_codes = keep.tile([P, N], U32, name="w2_codes", align_bytes=64)
-        w2_scale = keep.tile([P, N], U8, name="w2_scale", align_bytes=64)
+        def quantise_z(q):
+            nc.vector.quantize_mx(out=z_codes[q][:].bitcast(FP8X4), scales=z_scale[q][:], in_=z_bf16[q])
 
-        def cast_w2(g):
-            cols = slice(g * N // 2, (g + 1) * N // 2)
-            dst = w2_bf16[:].rearrange("p (c j) -> p c j", j=PACK)[:, cols, :].rearrange("p (c i) j -> p c j i", i=4)
-            src = w2_raw[:, :, cols].rearrange("p j (c i) -> p c j i", i=4)
-            nc.scalar.copy(dst, src)
+        def multiply(bank, m, q):
+            cols = slice((m % 2) * P, (m % 2 + 1) * P)
+            nc.tensor.matmul_mx(
+                out=bank[:, (q % 2) * QUARTER : (q % 2 + 1) * QUARTER],
+                lhsT=w2_codes[m // 2][:, cols].bitcast(FP8X4),
+                lhsT_scale=w2_scale[m // 2][:, cols],
+                rhs=z_codes[q][:].bitcast(FP8X4),
+                rhs_scale=z_scale[q][:],
+                start=True,
+                stop=True,
+            )
 
-        z_codes = [keep.tile([P, HALF], U32, name="z_codes_%d" % a, align_bytes=64) for a in range(2)]
-        z_scale = [keep.tile([P, HALF], U8, name="z_scale_%d" % a, align_bytes=64) for a in range(2)]
-
-        def quantise_z(a):
-            nc.vector.quantize_mx(out=z_codes[a][:].bitcast(FP8X4), scales=z_scale[a][:], in_=z_bf16[a])
-
-        def project(a, first, count, bank_tag, on_vector):
-            bank = psum.tile([P, count, HALF], F32, name="o_%d_%d" % (a, first), tag=bank_tag)
-            for e in range(count):
-                cols = slice((first + e) * P, (first + e + 1) * P)
-                nc.tensor.matmul_mx(
-                    out=bank[:, e, :],
-                    lhsT=w2_codes[:, cols].bitcast(FP8X4),
-                    lhsT_scale=w2_scale[:, cols],
-                    rhs=z_codes[a][:].bitcast(FP8X4),
-                    rhs_scale=z_scale[a][:],
-                    start=True,
-                    stop=True,
-                )
-            staged = keep.tile([P, count, HALF], F32, name="staged_%d_%d" % (a, first), align_bytes=64)
-            if on_vector:
-                nc.vector.tensor_copy(staged[:], bank[:])
-            else:
-                nc.scalar.copy(staged[:], bank[:])
-            rows = out[first * P : (first + count) * P, a * HALF : (a + 1) * HALF]
-            nc.sync.dma_start(rows.rearrange("(e p) n -> p e n", p=P), staged[:])
+        def project(a):
+            banks = [psum.tile([P, HALF], F32, name="o_%d_%d" % (a, m), tag=("out_%d" if a == 0 else "y_%d") % m) for m in range(PACK)]
+            for q in (2 * a, 2 * a + 1):
+                for m in range(PACK):
+                    multiply(banks[m], m, q)
+            for m in range(PACK):
+                staged = keep.tile([P, HALF], F32, name="staged_%d_%d" % (a, m), align_bytes=64)
+                if m % 2 == 1:
+                    nc.vector.tensor_copy(staged[:], banks[m][:])
+                else:
+                    nc.scalar.copy(staged[:], banks[m][:])
+                nc.sync.dma_start(out[m * P : (m + 1) * P, half(a)], staged[:])
 
         for t in range(PACK):
-            normalise(t)
-        for t in range(2):
-            for a in range(2):
-                scale_by_gamma(t, a)
-            for a in range(2):
-                shift_by_beta(t, a)
-        for g in range(2):
-            cast_w2(g)
-        z_all = keep.tile([P, S * PACK], BF16, name="z_all", tag="w2_then_z", align_bytes=64)
-        z_bf16 = [z_all[:, a * HALF * PACK : (a + 1) * HALF * PACK] for a in range(2)]
-        for a in range(2):
-            rectify(0, a, False)
-        scale_by_gamma(2, 0)
-        scale_by_gamma(2, 1)
-        scale_by_gamma(3, 0)
-        nc.vector.quantize_mx(out=w2_codes[:].bitcast(FP8X4), scales=w2_scale[:], in_=w2_bf16[:])
-        shift_by_beta(2, 0)
-        shift_by_beta(3, 0)
-        rectify(1, 0, False)
-        last = keep.tile([P, 3, HALF], F32, name="last", tag="scaled_3_0", align_bytes=64)
-        scaled[3, 1] = last[:, 0, :]
-        pre[1, 1] = last[:, 1:3, :]
-        scale_by_gamma(3, 1)
-        shift_by_beta(2, 1)
-        shift_by_beta(3, 1)
+            statistics(t)
+        for t in range(EARLY):
+            modulate_early(t)
+        w2_bf16 = keep.tile([P, N * PACK], BF16, name="w2_bf16", tag="small_%d" % EARLY, align_bytes=64)
+        scale_late(2, 0)
+        scale_late(2, 1)
+        shift_late(2, 0)
+        scale_late(3, 0)
+        shift_late(2, 1)
+        shift_late(3, 0)
+        quantise_w2(0)
+        scale_late(3, 1)
+        quantise_w2(1)
+        rectify(0, False)
+        rectify(1, False)
         quantise_z(0)
-        rectify(1, 1, True)
-        project(0, 0, 2, "out_0", False)
+        shift_late(3, 1)
         quantise_z(1)
-        project(0, 2, 2, "out_1", True)
-        for m in range(PACK):
-            project(1, m, 1, "y_%d" % m, m % 2 == 0)
+        rectify(3, False)
+        rectify(2, True)
+        quantise_z(2)
+        quantise_z(3)
+        project(0)
+        project(1)

@@ -55,8 +55,8 @@ def tile_picked_adain8_relu_p_kernel(tc, x_words, x_scales, w1, gamma, beta, w2,
             nc.sync.dma_start(gamma_sb[t][:], gamma_rows[:, t, :])
         nc.sync.dma_start(gamma_sb[2][:], gamma_rows[:, 2, :])
         nc.sync.dma_start(beta_sb[2][:], beta_rows[:, 2, :])
-        nc.sync.dma_start(w2_raw[:], w2.rearrange("(p j) c -> p j c", j=PACK))
         nc.sync.dma_start(gamma_sb[3][:], gamma_rows[:, 3, :])
+        nc.sync.dma_start(w2_raw[:], w2.rearrange("(p j) c -> p j c", j=PACK))
         nc.sync.dma_start(beta_sb[3][:], beta_rows[:, 3, :])
 
         x_scale = keep.tile([P, S], U8, name="x_scale", align_bytes=64)
@@ -95,17 +95,16 @@ def tile_picked_adain8_relu_p_kernel(tc, x_words, x_scales, w1, gamma, beta, w2,
             )
             y.append(bank)
 
-        unused = keep.tile([P, S], BF16, name="unused", align_bytes=64)
         neg_mean, rstd = {}, {}
         pre = [keep.tile([P, PACK, HALF], F32, name="pre_%d" % a, align_bytes=64) for a in range(2)]
-        h = {(t, a): keep.tile([P, HALF], F32, name="h_%d_%d" % (t, a), align_bytes=64)[:] for t, a in ((2, 0), (2, 1), (3, 1))}
-        h[3, 0] = pre[1][:, 2, :]
+        h = {(t, a): keep.tile([P, HALF], F32, name="h_%d_%d" % (t, a), align_bytes=64)[:] for t in range(EARLY, PACK) for a in range(2)}
 
         def half(a):
             return slice(a * HALF, (a + 1) * HALF)
 
         def statistics(t):
-            small = keep.tile([P, 4], F32, name="small_%d" % t, tag="small_%d" % min(t, EARLY), align_bytes=64)
+            small = keep.tile([P, 4], F32, name="small_%d" % t)
+            unused = keep.tile([P, S], BF16, name="unused_%d" % t, align_bytes=64)
             neg_mean[t], sum_sq, rstd[t], shift = small[:, 0:1], small[:, 1:2], small[:, 2:3], small[:, 3:4]
             nc.scalar.activation(unused[:], y[t][:], ACT.Copy, scale=-1.0 / S, accum_out=neg_mean[t])
             nc.scalar.activation(unused[:], y[t][:], ACT.Square, bias=neg_mean[t], accum_out=sum_sq)
@@ -152,8 +151,7 @@ def tile_picked_adain8_relu_p_kernel(tc, x_words, x_scales, w1, gamma, beta, w2,
             w2_codes.append(codes)
             w2_scale.append(scale)
 
-        z_bf16 = [pre[1][:, 3, :].bitcast(BF16)]
-        z_bf16.extend(keep.tile([P, QUARTER * PACK], BF16, name="z_bf16_%d" % q, align_bytes=64)[:] for q in range(1, 4))
+        z_bf16 = [keep.tile([P, QUARTER * PACK], BF16, name="z_bf16_%d" % q, align_bytes=64)[:] for q in range(4)]
         z_codes = [keep.tile([P, QUARTER], U32, name="z_codes_%d" % q, align_bytes=64) for q in range(4)]
         z_scale = [keep.tile([P, QUARTER], U8, name="z_scale_%d" % q, align_bytes=64) for q in range(4)]
 
@@ -187,7 +185,7 @@ def tile_picked_adain8_relu_p_kernel(tc, x_words, x_scales, w1, gamma, beta, w2,
                     multiply(banks[m], m, q)
             for m in range(PACK):
                 staged = keep.tile([P, HALF], F32, name="staged_%d_%d" % (a, m), align_bytes=64)
-                if m % 2 == 1:
+                if m % 2 == 0:
                     nc.vector.tensor_copy(staged[:], banks[m][:])
                 else:
                     nc.scalar.copy(staged[:], banks[m][:])
@@ -197,20 +195,20 @@ def tile_picked_adain8_relu_p_kernel(tc, x_words, x_scales, w1, gamma, beta, w2,
             statistics(t)
         for t in range(EARLY):
             modulate_early(t)
-        w2_bf16 = keep.tile([P, N * PACK], BF16, name="w2_bf16", tag="small_%d" % EARLY, align_bytes=64)
+        w2_bf16 = keep.tile([P, N * PACK], BF16, name="w2_bf16", align_bytes=64)
         scale_late(2, 0)
         scale_late(2, 1)
         shift_late(2, 0)
-        scale_late(3, 0)
         shift_late(2, 1)
-        shift_late(3, 0)
+        scale_late(3, 0)
         quantise_w2(0)
+        shift_late(3, 0)
         scale_late(3, 1)
         quantise_w2(1)
         rectify(0, False)
         rectify(1, False)
-        quantise_z(0)
         shift_late(3, 1)
+        quantise_z(0)
         quantise_z(1)
         rectify(3, False)
         rectify(2, True)

@@ -52,6 +52,7 @@ def tile_picked_adain8_relu_p_kernel(tc, x_words, x_scales, w1, gamma, beta, w2,
         nc.sync.dma_start(sty_sb[:], sty)
         for t in range(EARLY):
             nc.sync.dma_start(beta_sb[t][:], beta_rows[:, t, :])
+        for t in range(EARLY):
             nc.sync.dma_start(gamma_sb[t][:], gamma_rows[:, t, :])
         nc.sync.dma_start(gamma_sb[2][:], gamma_rows[:, 2, :])
         nc.sync.dma_start(beta_sb[2][:], beta_rows[:, 2, :])
@@ -119,9 +120,9 @@ def tile_picked_adain8_relu_p_kernel(tc, x_words, x_scales, w1, gamma, beta, w2,
         def styles(a):
             return sty_sb[:, a * HALF // 16 : (a + 1) * HALF // 16]
 
+        picked_beta = [keep.tile([P, S], F32, name="picked_beta_%d" % t, align_bytes=64) for t in range(EARLY)]
+
         def modulate_early(t):
-            picked_beta = keep.tile([P, S], F32, name="picked_beta_%d" % t, align_bytes=64)
-            nc.vector.tensor_copy(picked_beta[:], beta_sb[t][:].indirect(sty_sb[:]))
             picked_gamma = [keep.tile([P, HALF], F32, name="picked_gamma_%d_%d" % (t, a), align_bytes=64) for a in range(2)]
             for a in range(2):
                 nc.vector.tensor_copy(picked_gamma[a][:], gamma_sb[t][:].indirect(styles(a)))
@@ -129,7 +130,7 @@ def tile_picked_adain8_relu_p_kernel(tc, x_words, x_scales, w1, gamma, beta, w2,
                 scaled[t, a] = keep.tile([P, HALF], F32, name="scaled_%d_%d" % (t, a), align_bytes=64)
                 nc.vector.scalar_tensor_tensor(scaled[t, a][:], y[t][:, half(a)], neg_mean[t], picked_gamma[a][:], ALU.add, ALU.mult)
             for a in range(2):
-                nc.vector.scalar_tensor_tensor(pre[a][:, t, :], scaled[t, a][:], rstd[t], picked_beta[:, half(a)], ALU.mult, ALU.add)
+                nc.vector.scalar_tensor_tensor(pre[a][:, t, :], scaled[t, a][:], rstd[t], picked_beta[t][:, half(a)], ALU.mult, ALU.add)
 
         def scale_late(t, a):
             scaled[t, a] = keep.tile([P, HALF], F32, name="scaled_%d_%d" % (t, a), tag="scaled_3" if t == 3 else "scaled_2_%d" % a, align_bytes=64)
@@ -151,41 +152,44 @@ def tile_picked_adain8_relu_p_kernel(tc, x_words, x_scales, w1, gamma, beta, w2,
             w2_codes.append(codes)
             w2_scale.append(scale)
 
-        z_bf16 = [keep.tile([P, QUARTER * PACK], BF16, name="z_bf16_%d" % q, align_bytes=64)[:] for q in range(4)]
-        z_codes = [keep.tile([P, QUARTER], U32, name="z_codes_%d" % q, align_bytes=64) for q in range(4)]
-        z_scale = [keep.tile([P, QUARTER], U8, name="z_scale_%d" % q, align_bytes=64) for q in range(4)]
-
-        def rectify(q, on_vector):
-            dst = z_bf16[q].rearrange("p (c i t) -> p c t i", i=4, t=PACK)
-            src = pre[q // 2][:, :, (q % 2) * QUARTER : (q % 2 + 1) * QUARTER].rearrange("p t (c i) -> p c t i", i=4)
+        def rectify(places, on_vector, tag):
+            a, first, count = places.start // HALF, places.start % HALF, places.stop - places.start
+            z_bf16 = keep.tile([P, count * PACK], BF16, name="z_bf16_%d" % places.start, tag=tag, align_bytes=64)
+            dst = z_bf16[:].rearrange("p (c i t) -> p c t i", i=4, t=PACK)
+            src = pre[a][:, :, first : first + count].rearrange("p t (c i) -> p c t i", i=4)
             if on_vector:
                 nc.vector.tensor_scalar(dst, src, 0.0, None, ALU.max)
             else:
                 nc.scalar.activation(dst, src, ACT.Relu)
+            return z_bf16
 
-        def quantise_z(q):
-            nc.vector.quantize_mx(out=z_codes[q][:].bitcast(FP8X4), scales=z_scale[q][:], in_=z_bf16[q])
+        def quantise_z(z_bf16, label):
+            count = z_bf16.shape[1] // PACK
+            codes = keep.tile([P, count], U32, name="z_codes_" + label, align_bytes=64)
+            scale = keep.tile([P, count], U8, name="z_scale_" + label, align_bytes=64)
+            nc.vector.quantize_mx(out=codes[:].bitcast(FP8X4), scales=scale[:], in_=z_bf16[:])
+            return codes, scale
 
-        def multiply(bank, m, q):
-            cols = slice((m % 2) * P, (m % 2 + 1) * P)
-            nc.tensor.matmul_mx(
-                out=bank[:, (q % 2) * QUARTER : (q % 2 + 1) * QUARTER],
-                lhsT=w2_codes[m // 2][:, cols].bitcast(FP8X4),
-                lhsT_scale=w2_scale[m // 2][:, cols],
-                rhs=z_codes[q][:].bitcast(FP8X4),
-                rhs_scale=z_scale[q][:],
-                start=True,
-                stop=True,
-            )
-
-        def project(a):
+        def project(a, pieces, on_vector):
             banks = [psum.tile([P, HALF], F32, name="o_%d_%d" % (a, m), tag=("out_%d" if a == 0 else "y_%d") % m) for m in range(PACK)]
-            for q in (2 * a, 2 * a + 1):
+            first = 0
+            for codes, scale in pieces:
+                count = codes.shape[1]
                 for m in range(PACK):
-                    multiply(banks[m], m, q)
+                    cols = slice((m % 2) * P, (m % 2 + 1) * P)
+                    nc.tensor.matmul_mx(
+                        out=banks[m][:, first : first + count],
+                        lhsT=w2_codes[m // 2][:, cols].bitcast(FP8X4),
+                        lhsT_scale=w2_scale[m // 2][:, cols],
+                        rhs=codes[:].bitcast(FP8X4),
+                        rhs_scale=scale[:],
+                        start=True,
+                        stop=True,
+                    )
+                first = first + count
             for m in range(PACK):
                 staged = keep.tile([P, HALF], F32, name="staged_%d_%d" % (a, m), align_bytes=64)
-                if m % 2 == 0:
+                if m in on_vector:
                     nc.vector.tensor_copy(staged[:], banks[m][:])
                 else:
                     nc.scalar.copy(staged[:], banks[m][:])
@@ -193,6 +197,8 @@ def tile_picked_adain8_relu_p_kernel(tc, x_words, x_scales, w1, gamma, beta, w2,
 
         for t in range(PACK):
             statistics(t)
+        for t in range(EARLY):
+            nc.vector.tensor_copy(picked_beta[t][:], beta_sb[t][:].indirect(sty_sb[:]))
         for t in range(EARLY):
             modulate_early(t)
         w2_bf16 = keep.tile([P, N * PACK], BF16, name="w2_bf16", align_bytes=64)
@@ -205,14 +211,12 @@ def tile_picked_adain8_relu_p_kernel(tc, x_words, x_scales, w1, gamma, beta, w2,
         shift_late(3, 0)
         scale_late(3, 1)
         quantise_w2(1)
-        rectify(0, False)
-        rectify(1, False)
+        z_first = rectify(slice(0, HALF), False, "z_shared")
         shift_late(3, 1)
-        quantise_z(0)
-        quantise_z(1)
-        rectify(3, False)
-        rectify(2, True)
-        quantise_z(2)
-        quantise_z(3)
-        project(0)
-        project(1)
+        first_half = quantise_z(z_first, "first")
+        z_fourth = rectify(slice(HALF + QUARTER, S), False, "z_fourth")
+        z_third = rectify(slice(HALF, HALF + QUARTER), True, "z_shared")
+        third = quantise_z(z_third, "third")
+        fourth = quantise_z(z_fourth, "fourth")
+        project(0, [first_half], (2,))
+        project(1, [third, fourth], (0, 2))

@@ -18,7 +18,6 @@ ALU = mybir.AluOpType
 P = 128
 PACK = 4
 HALF = S // 2
-EPS = 1e-5
 EARLY = 2
 QUARTER = S // 4
 
@@ -41,9 +40,10 @@ def tile_picked_adain8_relu_p_kernel(tc, x_words, x_scales, w1, gamma, beta, w2,
         beta_rows = beta.rearrange("(p t) u -> p t u", t=PACK)
 
         nc.vector.memset(scale_table[:].bitcast(I32), 0)
-        warm = keep.tile([P, 2], F32, name="warm")
-        nc.vector.memset(warm[:, 0:1], 1.0)
-        nc.scalar.activation(warm[:, 1:2], warm[:, 0:1], ACT.Abs_reciprocal_sqrt)
+        consts = keep.tile([P, 2], F32, name="consts")
+        one, eps = consts[:, 0:1], consts[:, 1:2]
+        nc.vector.memset(one, 1.0)
+        nc.scalar.activation(eps, one, ACT.Abs_reciprocal_sqrt, scale=1e10)
         nc.sync.dma_start(w1_raw[:], w1.rearrange("(p j) c -> p j c", j=PACK))
         for r in range(4):
             nc.sync.dma_start(scale_table[r:P:32, :].bitcast(I32), x_scales[0, r:16:4, :].bitcast(I32))
@@ -55,8 +55,8 @@ def tile_picked_adain8_relu_p_kernel(tc, x_words, x_scales, w1, gamma, beta, w2,
         for t in range(EARLY):
             nc.sync.dma_start(gamma_sb[t][:], gamma_rows[:, t, :])
         nc.sync.dma_start(gamma_sb[2][:], gamma_rows[:, 2, :])
-        nc.sync.dma_start(beta_sb[2][:], beta_rows[:, 2, :])
         nc.sync.dma_start(gamma_sb[3][:], gamma_rows[:, 3, :])
+        nc.sync.dma_start(beta_sb[2][:], beta_rows[:, 2, :])
         nc.sync.dma_start(w2_raw[:], w2.rearrange("(p j) c -> p j c", j=PACK))
         nc.sync.dma_start(beta_sb[3][:], beta_rows[:, 3, :])
 
@@ -109,7 +109,7 @@ def tile_picked_adain8_relu_p_kernel(tc, x_words, x_scales, w1, gamma, beta, w2,
             neg_mean[t], sum_sq, rstd[t], shift = small[:, 0:1], small[:, 1:2], small[:, 2:3], small[:, 3:4]
             nc.scalar.activation(unused[:], y[t][:], ACT.Copy, scale=-1.0 / S, accum_out=neg_mean[t])
             nc.scalar.activation(unused[:], y[t][:], ACT.Square, bias=neg_mean[t], accum_out=sum_sq)
-            nc.scalar.activation(rstd[t], sum_sq, ACT.Abs_reciprocal_sqrt, scale=1.0 / S, bias=EPS)
+            nc.scalar.activation(rstd[t], sum_sq, ACT.Abs_reciprocal_sqrt, scale=1.0 / S, bias=eps)
             if t >= EARLY:
                 nc.scalar.activation(shift, rstd[t], ACT.Copy, scale=neg_mean[t])
                 for a in range(2):
@@ -204,11 +204,11 @@ def tile_picked_adain8_relu_p_kernel(tc, x_words, x_scales, w1, gamma, beta, w2,
         w2_bf16 = keep.tile([P, N * PACK], BF16, name="w2_bf16", align_bytes=64)
         scale_late(2, 0)
         scale_late(2, 1)
+        scale_late(3, 0)
         shift_late(2, 0)
         shift_late(2, 1)
-        scale_late(3, 0)
-        quantise_w2(0)
         shift_late(3, 0)
+        quantise_w2(0)
         scale_late(3, 1)
         quantise_w2(1)
         z_first = rectify(slice(0, HALF), False, "z_shared")

@@ -79,22 +79,31 @@ def tile_picked_adain8_relu_p_kernel(tc, x_words, x_scales, w1, gamma, beta, w2,
             w1_scale.append(scale)
 
         x_codes = keep.tile([P, S], U32, name="x_codes", align_bytes=64)
-        nc.vector.tensor_copy(x_codes[:], word_table[:].indirect(offs_sb[:]))
+        for a in range(2):
+            nc.vector.tensor_copy(x_codes[:, a * HALF : (a + 1) * HALF], word_table[:].indirect(offs_sb[:, a * HALF // 16 : (a + 1) * HALF // 16]))
+        y = [psum.tile([P, S], F32, name="y_%d" % t, tag="y_%d" % t) for t in range(PACK)]
+        folded = {t: psum.tile([P, P], F32, name="folded_%d" % t, tag="out_%d" % t) for t in range(EARLY, PACK)}
 
-        y = []
-        for t in range(PACK):
-            bank = psum.tile([P, S], F32, name="y_%d" % t, tag="y_%d" % t)
+        def first_product(t, target, places, start, stop):
             cols = slice((t % 2) * P, (t % 2 + 1) * P)
             nc.tensor.matmul_mx(
-                out=bank[:],
+                out=target,
                 lhsT=w1_codes[t // 2][:, cols].bitcast(FP8X4),
                 lhsT_scale=w1_scale[t // 2][:, cols],
-                rhs=x_codes[:].bitcast(FP8X4),
-                rhs_scale=x_scale[:],
-                start=True,
-                stop=True,
+                rhs=x_codes[:, places].bitcast(FP8X4),
+                rhs_scale=x_scale[:, places],
+                start=start,
+                stop=stop,
             )
-            y.append(bank)
+
+        for a in range(2):
+            places = slice(a * HALF, (a + 1) * HALF)
+            for t in range(EARLY):
+                first_product(t, y[t][:, places], places, True, True)
+        for t in range(EARLY, PACK):
+            for c in range(PACK):
+                first_product(t, folded[t][:], slice(c * P, (c + 1) * P), c == 0, c == PACK - 1)
+            first_product(t, y[t][:], slice(0, S), True, True)
 
         neg_mean, rstd = {}, {}
         pre = [keep.tile([P, PACK, HALF], F32, name="pre_%d" % a, align_bytes=64) for a in range(2)]
@@ -107,7 +116,10 @@ def tile_picked_adain8_relu_p_kernel(tc, x_words, x_scales, w1, gamma, beta, w2,
             small = keep.tile([P, 4], F32, name="small_%d" % t)
             unused = keep.tile([P, S], BF16, name="unused_%d" % t, align_bytes=64)
             neg_mean[t], sum_sq, rstd[t], shift = small[:, 0:1], small[:, 1:2], small[:, 2:3], small[:, 3:4]
-            nc.scalar.activation(unused[:], y[t][:], ACT.Copy, scale=-1.0 / S, accum_out=neg_mean[t])
+            if t < EARLY:
+                nc.scalar.activation(unused[:], y[t][:], ACT.Copy, scale=-1.0 / S, accum_out=neg_mean[t])
+            else:
+                nc.scalar.activation(unused[:, 0:P], folded[t][:], ACT.Copy, scale=-1.0 / S, accum_out=neg_mean[t])
             nc.scalar.activation(unused[:], y[t][:], ACT.Square, bias=neg_mean[t], accum_out=sum_sq)
             nc.scalar.activation(rstd[t], sum_sq, ACT.Abs_reciprocal_sqrt, scale=1.0 / S, bias=eps)
             if t >= EARLY:

@@ -79,8 +79,7 @@ def tile_picked_adain8_relu_p_kernel(tc, x_words, x_scales, w1, gamma, beta, w2,
             w1_scale.append(scale)
 
         x_codes = keep.tile([P, S], U32, name="x_codes", align_bytes=64)
-        for a in range(2):
-            nc.vector.tensor_copy(x_codes[:, a * HALF : (a + 1) * HALF], word_table[:].indirect(offs_sb[:, a * HALF // 16 : (a + 1) * HALF // 16]))
+        nc.vector.tensor_copy(x_codes[:], word_table[:].indirect(offs_sb[:]))
         y = [psum.tile([P, S], F32, name="y_%d" % t, tag="y_%d" % t) for t in range(PACK)]
         folded = {t: psum.tile([P, P], F32, name="folded_%d" % t, tag="out_%d" % t) for t in range(EARLY, PACK)}
 
@@ -96,10 +95,8 @@ def tile_picked_adain8_relu_p_kernel(tc, x_words, x_scales, w1, gamma, beta, w2,
                 stop=stop,
             )
 
-        for a in range(2):
-            places = slice(a * HALF, (a + 1) * HALF)
-            for t in range(EARLY):
-                first_product(t, y[t][:, places], places, True, True)
+        for t in range(EARLY):
+            first_product(t, y[t][:], slice(0, S), True, True)
         for t in range(EARLY, PACK):
             for c in range(PACK):
                 first_product(t, folded[t][:], slice(c * P, (c + 1) * P), c == 0, c == PACK - 1)

@@ -103,8 +103,10 @@ def tile_picked_adain8_relu_p_kernel(tc, x_words, x_scales, w1, gamma, beta, w2,
             first_product(t, y[t][:], slice(0, S), True, True)
 
         neg_mean, rstd = {}, {}
-        pre = [keep.tile([P, PACK, HALF], F32, name="pre_%d" % a, align_bytes=64) for a in range(2)]
+        pre = [keep.tile([P, PACK + a, HALF], F32, name="pre_%d" % a, align_bytes=64) for a in range(2)]
         h = {(t, a): keep.tile([P, HALF], F32, name="h_%d_%d" % (t, a), align_bytes=64)[:] for t in range(EARLY, PACK) for a in range(2)}
+
+        centred = keep.tile([P, S], F32, name="centred", align_bytes=64)
 
         def half(a):
             return slice(a * HALF, (a + 1) * HALF)
@@ -119,6 +121,8 @@ def tile_picked_adain8_relu_p_kernel(tc, x_words, x_scales, w1, gamma, beta, w2,
                 nc.scalar.activation(unused[:, 0:P], folded[t][:], ACT.Copy, scale=-1.0 / S, accum_out=neg_mean[t])
             nc.scalar.activation(unused[:], y[t][:], ACT.Square, bias=neg_mean[t], accum_out=sum_sq)
             nc.scalar.activation(rstd[t], sum_sq, ACT.Abs_reciprocal_sqrt, scale=1.0 / S, bias=eps)
+            if t == 1:
+                nc.scalar.activation(centred[:], y[t][:], ACT.Identity, bias=neg_mean[t])
             if t >= EARLY:
                 nc.scalar.activation(shift, rstd[t], ACT.Copy, scale=neg_mean[t])
                 for a in range(2):
@@ -132,12 +136,17 @@ def tile_picked_adain8_relu_p_kernel(tc, x_words, x_scales, w1, gamma, beta, w2,
         picked_beta = [keep.tile([P, S], F32, name="picked_beta_%d" % t, align_bytes=64) for t in range(EARLY)]
 
         def modulate_early(t):
-            picked_gamma = [keep.tile([P, HALF], F32, name="picked_gamma_%d_%d" % (t, a), align_bytes=64) for a in range(2)]
-            for a in range(2):
-                nc.vector.tensor_copy(picked_gamma[a][:], gamma_sb[t][:].indirect(styles(a)))
             for a in range(2):
                 scaled[t, a] = keep.tile([P, HALF], F32, name="scaled_%d_%d" % (t, a), align_bytes=64)
-                nc.vector.scalar_tensor_tensor(scaled[t, a][:], y[t][:, half(a)], neg_mean[t], picked_gamma[a][:], ALU.add, ALU.mult)
+            if t == 0:
+                picked_gamma = [keep.tile([P, HALF], F32, name="picked_gamma_%d" % a, align_bytes=64) for a in range(2)]
+                for a in range(2):
+                    nc.vector.tensor_copy(picked_gamma[a][:], gamma_sb[t][:].indirect(styles(a)))
+                for a in range(2):
+                    nc.vector.scalar_tensor_tensor(scaled[t, a][:], y[t][:, half(a)], neg_mean[t], picked_gamma[a][:], ALU.add, ALU.mult)
+            else:
+                for a in range(2):
+                    nc.vector.tensor_tensor(scaled[t, a][:], gamma_sb[t][:].indirect(styles(a)), centred[:, half(a)], ALU.mult)
             for a in range(2):
                 nc.vector.scalar_tensor_tensor(pre[a][:, t, :], scaled[t, a][:], rstd[t], picked_beta[t][:, half(a)], ALU.mult, ALU.add)
 
@@ -163,9 +172,12 @@ def tile_picked_adain8_relu_p_kernel(tc, x_words, x_scales, w1, gamma, beta, w2,
 
         def rectify(places, on_vector, tag):
             a, first, count = places.start // HALF, places.start % HALF, places.stop - places.start
-            z_bf16 = keep.tile([P, count * PACK], BF16, name="z_bf16_%d" % places.start, tag=tag, align_bytes=64)
-            dst = z_bf16[:].rearrange("p (c i t) -> p c t i", i=4, t=PACK)
-            src = pre[a][:, :, first : first + count].rearrange("p t (c i) -> p c t i", i=4)
+            if tag is None:
+                z_bf16 = pre[1][:, PACK - 1 :, :].rearrange("p r c -> p (r c)").bitcast(BF16)
+            else:
+                z_bf16 = keep.tile([P, count * PACK], BF16, name="z_bf16_%d" % places.start, tag=tag, align_bytes=64)[:]
+            dst = z_bf16.rearrange("p (c i t) -> p c t i", i=4, t=PACK)
+            src = pre[a][:, 0:PACK, first : first + count].rearrange("p t (c i) -> p c t i", i=4)
             if on_vector:
                 nc.vector.tensor_scalar(dst, src, 0.0, None, ALU.max)
             else:
@@ -176,33 +188,42 @@ def tile_picked_adain8_relu_p_kernel(tc, x_words, x_scales, w1, gamma, beta, w2,
             count = z_bf16.shape[1] // PACK
             codes = keep.tile([P, count], U32, name="z_codes_" + label, align_bytes=64)
             scale = keep.tile([P, count], U8, name="z_scale_" + label, align_bytes=64)
-            nc.vector.quantize_mx(out=codes[:].bitcast(FP8X4), scales=scale[:], in_=z_bf16[:])
+            nc.vector.quantize_mx(out=codes[:].bitcast(FP8X4), scales=scale[:], in_=z_bf16)
             return codes, scale
 
-        def project(a, pieces, on_vector):
-            banks = [psum.tile([P, HALF], F32, name="o_%d_%d" % (a, m), tag=("out_%d" if a == 0 else "y_%d") % m) for m in range(PACK)]
-            first = 0
-            for codes, scale in pieces:
-                count = codes.shape[1]
-                for m in range(PACK):
-                    cols = slice((m % 2) * P, (m % 2 + 1) * P)
-                    nc.tensor.matmul_mx(
-                        out=banks[m][:, first : first + count],
-                        lhsT=w2_codes[m // 2][:, cols].bitcast(FP8X4),
-                        lhsT_scale=w2_scale[m // 2][:, cols],
-                        rhs=codes[:].bitcast(FP8X4),
-                        rhs_scale=scale[:],
-                        start=True,
-                        stop=True,
-                    )
-                first = first + count
+        def second_product(target, m, codes, scale):
+            cols = slice((m % 2) * P, (m % 2 + 1) * P)
+            nc.tensor.matmul_mx(
+                out=target,
+                lhsT=w2_codes[m // 2][:, cols].bitcast(FP8X4),
+                lhsT_scale=w2_scale[m // 2][:, cols],
+                rhs=codes[:].bitcast(FP8X4),
+                rhs_scale=scale[:],
+                start=True,
+                stop=True,
+            )
+
+        def project_first_half(codes, scale):
             for m in range(PACK):
-                staged = keep.tile([P, HALF], F32, name="staged_%d_%d" % (a, m), align_bytes=64)
-                if m in on_vector:
-                    nc.vector.tensor_copy(staged[:], banks[m][:])
+                bank = psum.tile([P, HALF], F32, name="o_%d" % m, tag="out_%d" % m)
+                second_product(bank[:], m, codes, scale)
+                staged = keep.tile([P, HALF], F32, name="staged_%d" % m, align_bytes=64)
+                nc.scalar.copy(staged[:], bank[:])
+                nc.sync.dma_start(out[m * P : (m + 1) * P, half(0)], staged[:])
+
+        def project_quarter(q, codes, scale):
+            places = slice(HALF + q * QUARTER, HALF + (q + 1) * QUARTER)
+            for g in range(2):
+                bank = psum.tile([P, 2, QUARTER], F32, name="o_%d_%d" % (q, g), tag="y_%d" % (2 * q + g))
+                for i in range(2):
+                    second_product(bank[:, i, :], 2 * g + i, codes, scale)
+                staged = keep.tile([P, 2, QUARTER], F32, name="staged_%d_%d" % (q, g), align_bytes=64)
+                if g == 0:
+                    nc.scalar.copy(staged[:], bank[:])
                 else:
-                    nc.scalar.copy(staged[:], banks[m][:])
-                nc.sync.dma_start(out[m * P : (m + 1) * P, half(a)], staged[:])
+                    nc.vector.tensor_copy(staged[:], bank[:])
+                rows = out[2 * g * P : 2 * (g + 1) * P, places]
+                nc.sync.dma_start(rows.rearrange("(i p) c -> p i c", p=P), staged[:])
 
         for t in range(PACK):
             statistics(t)
@@ -220,12 +241,13 @@ def tile_picked_adain8_relu_p_kernel(tc, x_words, x_scales, w1, gamma, beta, w2,
         quantise_w2(0)
         scale_late(3, 1)
         quantise_w2(1)
-        z_first = rectify(slice(0, HALF), False, "z_shared")
-        shift_late(3, 1)
+        z_first = rectify(slice(0, HALF), False, None)
         first_half = quantise_z(z_first, "first")
-        z_fourth = rectify(slice(HALF + QUARTER, S), False, "z_fourth")
-        z_third = rectify(slice(HALF, HALF + QUARTER), True, "z_shared")
+        shift_late(3, 1)
+        z_third = rectify(slice(HALF, HALF + QUARTER), True, "z_third")
+        z_fourth = rectify(slice(HALF + QUARTER, S), True, "z_fourth")
         third = quantise_z(z_third, "third")
         fourth = quantise_z(z_fourth, "fourth")
-        project(0, [first_half], (2,))
-        project(1, [third, fourth], (0, 2))
+        project_first_half(*first_half)
+        project_quarter(0, *third)
+        project_quarter(1, *fourth)

@@ -18,8 +18,8 @@ ALU = mybir.AluOpType
 P = 128
 PACK = 4
 HALF = S // 2
-EARLY = 2
 QUARTER = S // 4
+EARLY = 2
 
 
 def tile_picked_adain8_relu_p_kernel(tc, x_words, x_scales, w1, gamma, beta, w2, offs, sty, out):
@@ -44,10 +44,13 @@ def tile_picked_adain8_relu_p_kernel(tc, x_words, x_scales, w1, gamma, beta, w2,
         one, eps = consts[:, 0:1], consts[:, 1:2]
         nc.vector.memset(one, 1.0)
         nc.scalar.activation(eps, one, ACT.Abs_reciprocal_sqrt, scale=1e10)
-        nc.sync.dma_start(w1_raw[:], w1.rearrange("(p j) c -> p j c", j=PACK))
+
+        w1_rows = w1.rearrange("(p j) c -> p j c", j=PACK)
+        nc.sync.dma_start(w1_raw[:, 0:2, :], w1_rows[:, 0:2, :])
         for r in range(4):
             nc.sync.dma_start(scale_table[r:P:32, :].bitcast(I32), x_scales[0, r:16:4, :].bitcast(I32))
         nc.sync.dma_start(offs_sb[:], offs)
+        nc.sync.dma_start(w1_raw[:, 2:4, :], w1_rows[:, 2:4, :])
         nc.sync.dma_start(word_table[:].bitcast(I32), x_words[0].rearrange("p n t -> p (n t)").bitcast(I32))
         nc.sync.dma_start(sty_sb[:], sty)
         for t in range(EARLY):
@@ -80,6 +83,7 @@ def tile_picked_adain8_relu_p_kernel(tc, x_words, x_scales, w1, gamma, beta, w2,
 
         x_codes = keep.tile([P, S], U32, name="x_codes", align_bytes=64)
         nc.vector.tensor_copy(x_codes[:], word_table[:].indirect(offs_sb[:]))
+
         y = [psum.tile([P, S], F32, name="y_%d" % t, tag="y_%d" % t) for t in range(PACK)]
         folded = {t: psum.tile([P, P], F32, name="folded_%d" % t, tag="out_%d" % t) for t in range(EARLY, PACK)}
 
@@ -105,7 +109,6 @@ def tile_picked_adain8_relu_p_kernel(tc, x_words, x_scales, w1, gamma, beta, w2,
         neg_mean, rstd = {}, {}
         pre = [keep.tile([P, PACK + a, HALF], F32, name="pre_%d" % a, align_bytes=64) for a in range(2)]
         h = {(t, a): keep.tile([P, HALF], F32, name="h_%d_%d" % (t, a), align_bytes=64)[:] for t in range(EARLY, PACK) for a in range(2)}
-
         centred = keep.tile([P, S], F32, name="centred", align_bytes=64)
 
         def half(a):
@@ -151,7 +154,8 @@ def tile_picked_adain8_relu_p_kernel(tc, x_words, x_scales, w1, gamma, beta, w2,
                 nc.vector.scalar_tensor_tensor(pre[a][:, t, :], scaled[t, a][:], rstd[t], picked_beta[t][:, half(a)], ALU.mult, ALU.add)
 
         def scale_late(t, a):
-            scaled[t, a] = keep.tile([P, HALF], F32, name="scaled_%d_%d" % (t, a), tag="scaled_3" if t == 3 else "scaled_2_%d" % a, align_bytes=64)
+            tag = "scaled_3" if t == 3 else "scaled_2_%d" % a
+            scaled[t, a] = keep.tile([P, HALF], F32, name="scaled_%d_%d" % (t, a), tag=tag, align_bytes=64)
             nc.vector.tensor_tensor(scaled[t, a][:], gamma_sb[t][:].indirect(styles(a)), h[t, a], ALU.mult)
 
         def shift_late(t, a):
@@ -170,19 +174,14 @@ def tile_picked_adain8_relu_p_kernel(tc, x_words, x_scales, w1, gamma, beta, w2,
             w2_codes.append(codes)
             w2_scale.append(scale)
 
-        def rectify(places, on_vector, tag):
+        def rectify(places, z_bf16, on_vector):
             a, first, count = places.start // HALF, places.start % HALF, places.stop - places.start
-            if tag is None:
-                z_bf16 = pre[1][:, PACK - 1 :, :].rearrange("p r c -> p (r c)").bitcast(BF16)
-            else:
-                z_bf16 = keep.tile([P, count * PACK], BF16, name="z_bf16_%d" % places.start, tag=tag, align_bytes=64)[:]
             dst = z_bf16.rearrange("p (c i t) -> p c t i", i=4, t=PACK)
             src = pre[a][:, 0:PACK, first : first + count].rearrange("p t (c i) -> p c t i", i=4)
             if on_vector:
                 nc.vector.tensor_scalar(dst, src, 0.0, None, ALU.max)
             else:
                 nc.scalar.activation(dst, src, ACT.Relu)
-            return z_bf16
 
         def quantise_z(z_bf16, label):
             count = z_bf16.shape[1] // PACK
@@ -241,13 +240,16 @@ def tile_picked_adain8_relu_p_kernel(tc, x_words, x_scales, w1, gamma, beta, w2,
         quantise_w2(0)
         scale_late(3, 1)
         quantise_w2(1)
-        z_first = rectify(slice(0, HALF), False, None)
+        z_first = pre[1][:, PACK - 1 :, :].rearrange("p r c -> p (r c)").bitcast(BF16)
+        rectify(slice(0, HALF), z_first, on_vector=False)
         first_half = quantise_z(z_first, "first")
         shift_late(3, 1)
-        z_third = rectify(slice(HALF, HALF + QUARTER), True, "z_third")
-        z_fourth = rectify(slice(HALF + QUARTER, S), True, "z_fourth")
-        third = quantise_z(z_third, "third")
-        fourth = quantise_z(z_fourth, "fourth")
+        z_last = []
+        for q in range(2):
+            z_quarter = keep.tile([P, QUARTER * PACK], BF16, name="z_bf16_%d" % q, align_bytes=64)
+            rectify(slice(HALF + q * QUARTER, HALF + (q + 1) * QUARTER), z_quarter[:], on_vector=True)
+            z_last.append(z_quarter[:])
+        last_quarters = [quantise_z(z_last[q], "quarter_%d" % q) for q in range(2)]
         project_first_half(*first_half)
-        project_quarter(0, *third)
-        project_quarter(1, *fourth)
+        for q in range(2):
+            project_quarter(q, *last_quarters[q])

@@ -33,7 +33,11 @@ def tile_picked_adain8_relu_p_kernel(tc, x_words, x_scales, w1, gamma, beta, w2,
         word_table = keep.tile([P, T], U32, name="word_table", align_bytes=64)
         scale_table = keep.tile([P, T], U8, name="scale_table", align_bytes=64)
         w1_raw = keep.tile([P, PACK, H], F32, name="w1_raw", align_bytes=64)
-        w2_raw = keep.tile([P, PACK, N], F32, name="w2_raw", align_bytes=64)
+        w2_parts = (slice(0, N - P), slice(N - P, N))
+        second = keep.tile([P, 3 * HALF], F32, name="second", align_bytes=64)
+        w2_first = keep.tile([P, PACK, N - P], F32, name="w2_first", align_bytes=64)
+        w2_raw = [w2_first[:], second[:].rearrange("p (j c) -> p j c", j=PACK)[:, :, :P]]
+        w2_rows = w2.rearrange("(p j) c -> p j c", j=PACK)
         gamma_sb = [keep.tile([P, U], F32, name="gamma_%d" % t, align_bytes=64) for t in range(PACK)]
         beta_sb = [keep.tile([P, U], F32, name="beta_%d" % t, align_bytes=64) for t in range(PACK)]
         gamma_rows = gamma.rearrange("(p t) u -> p t u", t=PACK)
@@ -59,9 +63,10 @@ def tile_picked_adain8_relu_p_kernel(tc, x_words, x_scales, w1, gamma, beta, w2,
             nc.sync.dma_start(gamma_sb[t][:], gamma_rows[:, t, :])
         nc.sync.dma_start(gamma_sb[2][:], gamma_rows[:, 2, :])
         nc.sync.dma_start(gamma_sb[3][:], gamma_rows[:, 3, :])
+        nc.sync.dma_start(w2_raw[0], w2_rows[:, :, w2_parts[0]])
         nc.sync.dma_start(beta_sb[2][:], beta_rows[:, 2, :])
-        nc.sync.dma_start(w2_raw[:], w2.rearrange("(p j) c -> p j c", j=PACK))
         nc.sync.dma_start(beta_sb[3][:], beta_rows[:, 3, :])
+        nc.sync.dma_start(w2_raw[1], w2_rows[:, :, w2_parts[1]])
 
         x_scale = keep.tile([P, S], U8, name="x_scale", align_bytes=64)
         nc.vector.tensor_copy(x_scale[:], scale_table[:].indirect(offs_sb[:]))
@@ -107,17 +112,24 @@ def tile_picked_adain8_relu_p_kernel(tc, x_words, x_scales, w1, gamma, beta, w2,
             first_product(t, y[t][:], slice(0, S), True, True)
 
         neg_mean, rstd = {}, {}
-        pre = [keep.tile([P, PACK + a, HALF], F32, name="pre_%d" % a, align_bytes=64) for a in range(2)]
+        sums = keep.tile([P, PACK * PACK, HALF], F32, name="sums", align_bytes=64)
+        pre = [sums[:, PACK * (PACK - 1) :, :], sums[:, PACK - 1 :: PACK, :]]
         h = {(t, a): keep.tile([P, HALF], F32, name="h_%d_%d" % (t, a), align_bytes=64)[:] for t in range(EARLY, PACK) for a in range(2)}
         centred = keep.tile([P, S], F32, name="centred", align_bytes=64)
 
         def half(a):
             return slice(a * HALF, (a + 1) * HALF)
 
+        shifts = {}
+
+        def normalise(t, a):
+            nc.scalar.activation(h[t, a], y[t][:, half(a)], ACT.Identity, scale=rstd[t], bias=shifts[t])
+
         def statistics(t):
             small = keep.tile([P, 4], F32, name="small_%d" % t)
             unused = keep.tile([P, S], BF16, name="unused_%d" % t, align_bytes=64)
-            neg_mean[t], sum_sq, rstd[t], shift = small[:, 0:1], small[:, 1:2], small[:, 2:3], small[:, 3:4]
+            mean_tile = keep.tile([P, 1], F32, name="mean_%d" % t, tag="w2_bf16" if t == 3 else "mean_%d" % t, align_bytes=64)
+            neg_mean[t], sum_sq, rstd[t], shift = mean_tile[:], small[:, 1:2], small[:, 2:3], small[:, 3:4]
             if t < EARLY:
                 nc.scalar.activation(unused[:], y[t][:], ACT.Copy, scale=-1.0 / S, accum_out=neg_mean[t])
             else:
@@ -128,8 +140,10 @@ def tile_picked_adain8_relu_p_kernel(tc, x_words, x_scales, w1, gamma, beta, w2,
                 nc.scalar.activation(centred[:], y[t][:], ACT.Identity, bias=neg_mean[t])
             if t >= EARLY:
                 nc.scalar.activation(shift, rstd[t], ACT.Copy, scale=neg_mean[t])
+                shifts[t] = shift
                 for a in range(2):
-                    nc.scalar.activation(h[t, a], y[t][:, half(a)], ACT.Identity, scale=rstd[t], bias=shift)
+                    if (t, a) in h:
+                        normalise(t, a)
 
         scaled = {}
 
@@ -154,25 +168,23 @@ def tile_picked_adain8_relu_p_kernel(tc, x_words, x_scales, w1, gamma, beta, w2,
                 nc.vector.scalar_tensor_tensor(pre[a][:, t, :], scaled[t, a][:], rstd[t], picked_beta[t][:, half(a)], ALU.mult, ALU.add)
 
         def scale_late(t, a):
-            tag = "scaled_3" if t == 3 else "scaled_2_%d" % a
-            scaled[t, a] = keep.tile([P, HALF], F32, name="scaled_%d_%d" % (t, a), tag=tag, align_bytes=64)
-            nc.vector.tensor_tensor(scaled[t, a][:], gamma_sb[t][:].indirect(styles(a)), h[t, a], ALU.mult)
+            if (t, a) == (3, 1):
+                scaled[t, a] = second[:, :HALF]
+            else:
+                scaled[t, a] = keep.tile([P, HALF], F32, name="scaled_%d_%d" % (t, a), align_bytes=64)[:]
+            nc.vector.tensor_tensor(scaled[t, a], gamma_sb[t][:].indirect(styles(a)), h[t, a], ALU.mult)
 
         def shift_late(t, a):
-            nc.vector.tensor_tensor(pre[a][:, t, :], beta_sb[t][:].indirect(styles(a)), scaled[t, a][:], ALU.add)
+            nc.vector.tensor_tensor(pre[a][:, t, :], beta_sb[t][:].indirect(styles(a)), scaled[t, a], ALU.add)
 
-        w2_codes, w2_scale = [], []
+        w2_codes = keep.tile([P, N], U32, name="w2_codes", align_bytes=64)
+        w2_scale = keep.tile([P, N], U8, name="w2_scale", align_bytes=64)
 
-        def quantise_w2(g):
-            grouped = w2_bf16[:, g * 2 * P * PACK : (g + 1) * 2 * P * PACK]
-            dst = grouped.rearrange("p (c i j) -> p c j i", i=4, j=PACK)
-            src = w2_raw[:, :, 2 * g * P : 2 * (g + 1) * P].rearrange("p j (c i) -> p c j i", i=4)
-            nc.scalar.copy(dst, src)
-            codes = keep.tile([P, 2 * P], U32, name="w2_codes_%d" % g, align_bytes=64)
-            scale = keep.tile([P, 2 * P], U8, name="w2_scale_%d" % g, align_bytes=64)
-            nc.vector.quantize_mx(out=codes[:].bitcast(FP8X4), scales=scale[:], in_=grouped)
-            w2_codes.append(codes)
-            w2_scale.append(scale)
+        def cast_w2():
+            for g, c in enumerate(w2_parts):
+                dst = w2_bf16[:, PACK * c.start : PACK * c.stop].rearrange("p (c i j) -> p c j i", i=4, j=PACK)
+                src = w2_raw[g].rearrange("p j (c i) -> p c j i", i=4)
+                nc.scalar.copy(dst, src)
 
         def rectify(places, z_bf16, on_vector):
             a, first, count = places.start // HALF, places.start % HALF, places.stop - places.start
@@ -191,11 +203,11 @@ def tile_picked_adain8_relu_p_kernel(tc, x_words, x_scales, w1, gamma, beta, w2,
             return codes, scale
 
         def second_product(target, m, codes, scale):
-            cols = slice((m % 2) * P, (m % 2 + 1) * P)
+            cols = slice(m * P, (m + 1) * P)
             nc.tensor.matmul_mx(
                 out=target,
-                lhsT=w2_codes[m // 2][:, cols].bitcast(FP8X4),
-                lhsT_scale=w2_scale[m // 2][:, cols],
+                lhsT=w2_codes[:, cols].bitcast(FP8X4),
+                lhsT_scale=w2_scale[:, cols],
                 rhs=codes[:].bitcast(FP8X4),
                 rhs_scale=scale[:],
                 start=True,
@@ -230,19 +242,25 @@ def tile_picked_adain8_relu_p_kernel(tc, x_words, x_scales, w1, gamma, beta, w2,
             nc.vector.tensor_copy(picked_beta[t][:], beta_sb[t][:].indirect(sty_sb[:]))
         for t in range(EARLY):
             modulate_early(t)
-        w2_bf16 = keep.tile([P, N * PACK], BF16, name="w2_bf16", align_bytes=64)
+        w2_bf16 = keep.tile([P, N * PACK], BF16, name="w2_bf16", tag="w2_bf16", align_bytes=64)
         scale_late(2, 0)
         scale_late(2, 1)
         scale_late(3, 0)
         shift_late(2, 0)
         shift_late(2, 1)
         shift_late(3, 0)
-        quantise_w2(0)
+        cast_w2()
+        nc.vector.quantize_mx(out=w2_codes[:].bitcast(FP8X4), scales=w2_scale[:], in_=w2_bf16[:])
         scale_late(3, 1)
-        quantise_w2(1)
-        z_first = pre[1][:, PACK - 1 :, :].rearrange("p r c -> p (r c)").bitcast(BF16)
-        rectify(slice(0, HALF), z_first, on_vector=False)
-        first_half = quantise_z(z_first, "first")
+        z_first = second[:, HALF:].bitcast(BF16)
+        first_codes = keep.tile([P, HALF], U32, name="z_codes_first", align_bytes=64)
+        first_scale = keep.tile([P, HALF], U8, name="z_scale_first", align_bytes=64)
+        for q in range(2):
+            places = slice(q * QUARTER, (q + 1) * QUARTER)
+            z_part = z_first[:, PACK * places.start : PACK * places.stop]
+            rectify(places, z_part, on_vector=False)
+            nc.vector.quantize_mx(out=first_codes[:, places].bitcast(FP8X4), scales=first_scale[:, places], in_=z_part)
+        first_half = (first_codes, first_scale)
         shift_late(3, 1)
         z_last = []
         for q in range(2):

@@ -20,6 +20,8 @@ PACK = 4
 HALF = S // 2
 QUARTER = S // 4
 EARLY = 2
+W1_SPLIT = 88
+LATE = 64
 
 
 def tile_picked_adain8_relu_p_kernel(tc, x_words, x_scales, w1, gamma, beta, w2, offs, sty, out):
@@ -33,10 +35,10 @@ def tile_picked_adain8_relu_p_kernel(tc, x_words, x_scales, w1, gamma, beta, w2,
         word_table = keep.tile([P, T], U32, name="word_table", align_bytes=64)
         scale_table = keep.tile([P, T], U8, name="scale_table", align_bytes=64)
         w1_raw = keep.tile([P, PACK, H], F32, name="w1_raw", align_bytes=64)
-        w2_parts = (slice(0, N - P), slice(N - P, N))
+        w2_parts = (slice(0, N - LATE), slice(N - LATE, N))
         second = keep.tile([P, 3 * HALF], F32, name="second", align_bytes=64)
-        w2_first = keep.tile([P, PACK, N - P], F32, name="w2_first", align_bytes=64)
-        w2_raw = [w2_first[:], second[:].rearrange("p (j c) -> p j c", j=PACK)[:, :, :P]]
+        w2_first = keep.tile([P, PACK, N - LATE], F32, name="w2_first", align_bytes=64)
+        w2_raw = [w2_first[:], second[:].rearrange("p (j c) -> p j c", j=PACK)[:, :, :LATE]]
         w2_rows = w2.rearrange("(p j) c -> p j c", j=PACK)
         gamma_sb = [keep.tile([P, U], F32, name="gamma_%d" % t, align_bytes=64) for t in range(PACK)]
         beta_sb = [keep.tile([P, U], F32, name="beta_%d" % t, align_bytes=64) for t in range(PACK)]
@@ -71,18 +73,16 @@ def tile_picked_adain8_relu_p_kernel(tc, x_words, x_scales, w1, gamma, beta, w2,
         x_scale = keep.tile([P, S], U8, name="x_scale", align_bytes=64)
         nc.vector.tensor_copy(x_scale[:], scale_table[:].indirect(offs_sb[:]))
 
+        w1_bf16 = keep.tile([P, H * PACK], BF16, name="w1_bf16", align_bytes=64)
+        dst = w1_bf16[:].rearrange("p (t m j) -> p m j t", t=PACK, j=PACK)
+        src = w1_raw[:].rearrange("p j (m t) -> p m j t", t=PACK)
+        nc.vector.tensor_copy(dst[:, :W1_SPLIT], src[:, :W1_SPLIT])
+        nc.scalar.copy(dst[:, W1_SPLIT:], src[:, W1_SPLIT:])
         w1_codes, w1_scale = [], []
         for u in range(2):
-            grouped = keep.tile([P, 2 * P * PACK], BF16, name="w1_bf16_%d" % u, align_bytes=64)
-            dst = grouped[:].rearrange("p (t m j) -> p m t j", t=2, j=PACK)
-            src = w1_raw[:].rearrange("p j (m t) -> p m t j", t=PACK)[:, :, 2 * u : 2 * u + 2, :]
-            if u == 0:
-                nc.vector.tensor_copy(dst, src)
-            else:
-                nc.scalar.copy(dst, src)
             codes = keep.tile([P, 2 * P], U32, name="w1_codes_%d" % u, align_bytes=64)
             scale = keep.tile([P, 2 * P], U8, name="w1_scale_%d" % u, align_bytes=64)
-            nc.vector.quantize_mx(out=codes[:].bitcast(FP8X4), scales=scale[:], in_=grouped[:])
+            nc.vector.quantize_mx(out=codes[:].bitcast(FP8X4), scales=scale[:], in_=w1_bf16[:, u * 2 * P * PACK : (u + 1) * 2 * P * PACK])
             w1_codes.append(codes)
             w1_scale.append(scale)
 
@@ -112,8 +112,14 @@ def tile_picked_adain8_relu_p_kernel(tc, x_words, x_scales, w1, gamma, beta, w2,
             first_product(t, y[t][:], slice(0, S), True, True)
 
         neg_mean, rstd = {}, {}
-        sums = keep.tile([P, PACK * PACK, HALF], F32, name="sums", align_bytes=64)
-        pre = [sums[:, PACK * (PACK - 1) :, :], sums[:, PACK - 1 :: PACK, :]]
+        pitch = (S, 3 * S + QUARTER)
+        last_row = 3 * pitch[1]
+        first_row = last_row + QUARTER - 3 * pitch[0]
+        sums = keep.tile([P, PACK * pitch[1]], F32, name="sums", align_bytes=64)
+        pre = [
+            sums[:, start : start + PACK * pitch[a]].rearrange("p (t c) -> p t c", t=PACK)[:, :, :HALF]
+            for a, start in enumerate((first_row, 0))
+        ]
         h = {(t, a): keep.tile([P, HALF], F32, name="h_%d_%d" % (t, a), align_bytes=64)[:] for t in range(EARLY, PACK) for a in range(2)}
         centred = keep.tile([P, S], F32, name="centred", align_bytes=64)
 
@@ -208,16 +214,19 @@ def tile_picked_adain8_relu_p_kernel(tc, x_words, x_scales, w1, gamma, beta, w2,
                 out=target,
                 lhsT=w2_codes[:, cols].bitcast(FP8X4),
                 lhsT_scale=w2_scale[:, cols],
-                rhs=codes[:].bitcast(FP8X4),
-                rhs_scale=scale[:],
+                rhs=codes.bitcast(FP8X4),
+                rhs_scale=scale,
                 start=True,
                 stop=True,
             )
 
         def project_first_half(codes, scale):
-            for m in range(PACK):
-                bank = psum.tile([P, HALF], F32, name="o_%d" % m, tag="out_%d" % m)
-                second_product(bank[:], m, codes, scale)
+            banks = [psum.tile([P, HALF], F32, name="o_%d" % m, tag="out_%d" % m) for m in range(PACK)]
+            for q in range(2):
+                places = slice(q * QUARTER, (q + 1) * QUARTER)
+                for m in range(PACK):
+                    second_product(banks[m][:, places], m, codes[:, places], scale[:, places])
+            for m, bank in enumerate(banks):
                 staged = keep.tile([P, HALF], F32, name="staged_%d" % m, align_bytes=64)
                 nc.scalar.copy(staged[:], bank[:])
                 nc.sync.dma_start(out[m * P : (m + 1) * P, half(0)], staged[:])
@@ -227,7 +236,7 @@ def tile_picked_adain8_relu_p_kernel(tc, x_words, x_scales, w1, gamma, beta, w2,
             for g in range(2):
                 bank = psum.tile([P, 2, QUARTER], F32, name="o_%d_%d" % (q, g), tag="y_%d" % (2 * q + g))
                 for i in range(2):
-                    second_product(bank[:, i, :], 2 * g + i, codes, scale)
+                    second_product(bank[:, i, :], 2 * g + i, codes[:], scale[:])
                 staged = keep.tile([P, 2, QUARTER], F32, name="staged_%d_%d" % (q, g), align_bytes=64)
                 if g == 0:
                     nc.scalar.copy(staged[:], bank[:])
@@ -255,18 +264,23 @@ def tile_picked_adain8_relu_p_kernel(tc, x_words, x_scales, w1, gamma, beta, w2,
         z_first = second[:, HALF:].bitcast(BF16)
         first_codes = keep.tile([P, HALF], U32, name="z_codes_first", align_bytes=64)
         first_scale = keep.tile([P, HALF], U8, name="z_scale_first", align_bytes=64)
+        z_parts = []
         for q in range(2):
             places = slice(q * QUARTER, (q + 1) * QUARTER)
             z_part = z_first[:, PACK * places.start : PACK * places.stop]
             rectify(places, z_part, on_vector=False)
+            z_parts.append((places, z_part))
+        for q, (places, z_part) in enumerate(z_parts):
+            if q == 1:
+                shift_late(3, 1)
             nc.vector.quantize_mx(out=first_codes[:, places].bitcast(FP8X4), scales=first_scale[:, places], in_=z_part)
         first_half = (first_codes, first_scale)
-        shift_late(3, 1)
         z_last = []
         for q in range(2):
-            z_quarter = keep.tile([P, QUARTER * PACK], BF16, name="z_bf16_%d" % q, align_bytes=64)
-            rectify(slice(HALF + q * QUARTER, HALF + (q + 1) * QUARTER), z_quarter[:], on_vector=True)
-            z_last.append(z_quarter[:])
+            start = first_row + q * pitch[0] + QUARTER
+            z_quarter = sums[:, start : start + HALF].bitcast(BF16)
+            rectify(slice(HALF + q * QUARTER, HALF + (q + 1) * QUARTER), z_quarter, on_vector=True)
+            z_last.append(z_quarter)
         last_quarters = [quantise_z(z_last[q], "quarter_%d" % q) for q in range(2)]
         project_first_half(*first_half)
         for q in range(2):

@@ -21,7 +21,7 @@ HALF = S // 2
 QUARTER = S // 4
 EARLY = 2
 W1_SPLIT = 88
-LATE = 64
+LATE = 32
 
 
 def tile_picked_adain8_relu_p_kernel(tc, x_words, x_scales, w1, gamma, beta, w2, offs, sty, out):
@@ -36,9 +36,9 @@ def tile_picked_adain8_relu_p_kernel(tc, x_words, x_scales, w1, gamma, beta, w2,
         scale_table = keep.tile([P, T], U8, name="scale_table", align_bytes=64)
         w1_raw = keep.tile([P, PACK, H], F32, name="w1_raw", align_bytes=64)
         w2_parts = (slice(0, N - LATE), slice(N - LATE, N))
-        second = keep.tile([P, 3 * HALF], F32, name="second", align_bytes=64)
+        reused = keep.tile([P, 3 * HALF], F32, name="reused", align_bytes=64)
         w2_first = keep.tile([P, PACK, N - LATE], F32, name="w2_first", align_bytes=64)
-        w2_raw = [w2_first[:], second[:].rearrange("p (j c) -> p j c", j=PACK)[:, :, :LATE]]
+        w2_raw = [w2_first[:], reused[:].rearrange("p (j c) -> p j c", j=PACK)[:, :, :LATE]]
         w2_rows = w2.rearrange("(p j) c -> p j c", j=PACK)
         gamma_sb = [keep.tile([P, U], F32, name="gamma_%d" % t, align_bytes=64) for t in range(PACK)]
         beta_sb = [keep.tile([P, U], F32, name="beta_%d" % t, align_bytes=64) for t in range(PACK)]
@@ -64,8 +64,8 @@ def tile_picked_adain8_relu_p_kernel(tc, x_words, x_scales, w1, gamma, beta, w2,
         for t in range(EARLY):
             nc.sync.dma_start(gamma_sb[t][:], gamma_rows[:, t, :])
         nc.sync.dma_start(gamma_sb[2][:], gamma_rows[:, 2, :])
-        nc.sync.dma_start(gamma_sb[3][:], gamma_rows[:, 3, :])
         nc.sync.dma_start(w2_raw[0], w2_rows[:, :, w2_parts[0]])
+        nc.sync.dma_start(gamma_sb[3][:], gamma_rows[:, 3, :])
         nc.sync.dma_start(beta_sb[2][:], beta_rows[:, 2, :])
         nc.sync.dma_start(beta_sb[3][:], beta_rows[:, 3, :])
         nc.sync.dma_start(w2_raw[1], w2_rows[:, :, w2_parts[1]])
@@ -126,16 +126,11 @@ def tile_picked_adain8_relu_p_kernel(tc, x_words, x_scales, w1, gamma, beta, w2,
         def half(a):
             return slice(a * HALF, (a + 1) * HALF)
 
-        shifts = {}
-
-        def normalise(t, a):
-            nc.scalar.activation(h[t, a], y[t][:, half(a)], ACT.Identity, scale=rstd[t], bias=shifts[t])
-
         def statistics(t):
-            small = keep.tile([P, 4], F32, name="small_%d" % t)
+            small = keep.tile([P, 3], F32, name="small_%d" % t)
             unused = keep.tile([P, S], BF16, name="unused_%d" % t, align_bytes=64)
             mean_tile = keep.tile([P, 1], F32, name="mean_%d" % t, tag="w2_bf16" if t == 3 else "mean_%d" % t, align_bytes=64)
-            neg_mean[t], sum_sq, rstd[t], shift = mean_tile[:], small[:, 1:2], small[:, 2:3], small[:, 3:4]
+            neg_mean[t], sum_sq, rstd[t], shift = mean_tile[:], small[:, 0:1], small[:, 1:2], small[:, 2:3]
             if t < EARLY:
                 nc.scalar.activation(unused[:], y[t][:], ACT.Copy, scale=-1.0 / S, accum_out=neg_mean[t])
             else:
@@ -146,10 +141,8 @@ def tile_picked_adain8_relu_p_kernel(tc, x_words, x_scales, w1, gamma, beta, w2,
                 nc.scalar.activation(centred[:], y[t][:], ACT.Identity, bias=neg_mean[t])
             if t >= EARLY:
                 nc.scalar.activation(shift, rstd[t], ACT.Copy, scale=neg_mean[t])
-                shifts[t] = shift
                 for a in range(2):
-                    if (t, a) in h:
-                        normalise(t, a)
+                    nc.scalar.activation(h[t, a], y[t][:, half(a)], ACT.Identity, scale=rstd[t], bias=shift)
 
         scaled = {}
 
@@ -175,7 +168,7 @@ def tile_picked_adain8_relu_p_kernel(tc, x_words, x_scales, w1, gamma, beta, w2,
 
         def scale_late(t, a):
             if (t, a) == (3, 1):
-                scaled[t, a] = second[:, :HALF]
+                scaled[t, a] = reused[:, :HALF]
             else:
                 scaled[t, a] = keep.tile([P, HALF], F32, name="scaled_%d_%d" % (t, a), align_bytes=64)[:]
             nc.vector.tensor_tensor(scaled[t, a], gamma_sb[t][:].indirect(styles(a)), h[t, a], ALU.mult)
@@ -261,27 +254,28 @@ def tile_picked_adain8_relu_p_kernel(tc, x_words, x_scales, w1, gamma, beta, w2,
         cast_w2()
         nc.vector.quantize_mx(out=w2_codes[:].bitcast(FP8X4), scales=w2_scale[:], in_=w2_bf16[:])
         scale_late(3, 1)
-        z_first = second[:, HALF:].bitcast(BF16)
+        z_first = reused[:, HALF:].bitcast(BF16)
         first_codes = keep.tile([P, HALF], U32, name="z_codes_first", align_bytes=64)
         first_scale = keep.tile([P, HALF], U8, name="z_scale_first", align_bytes=64)
-        z_parts = []
-        for q in range(2):
-            places = slice(q * QUARTER, (q + 1) * QUARTER)
-            z_part = z_first[:, PACK * places.start : PACK * places.stop]
-            rectify(places, z_part, on_vector=False)
-            z_parts.append((places, z_part))
-        for q, (places, z_part) in enumerate(z_parts):
-            if q == 1:
-                shift_late(3, 1)
-            nc.vector.quantize_mx(out=first_codes[:, places].bitcast(FP8X4), scales=first_scale[:, places], in_=z_part)
-        first_half = (first_codes, first_scale)
+        quarters = [slice(q * QUARTER, (q + 1) * QUARTER) for q in range(PACK)]
+
+        def quantise_first(q):
+            places = quarters[q]
+            z_bf16 = z_first[:, PACK * places.start : PACK * places.stop]
+            nc.vector.quantize_mx(out=first_codes[:, places].bitcast(FP8X4), scales=first_scale[:, places], in_=z_bf16)
+
+        for places in quarters[:2]:
+            rectify(places, z_first[:, PACK * places.start : PACK * places.stop], on_vector=False)
+        quantise_first(0)
+        shift_late(3, 1)
+        quantise_first(1)
         z_last = []
         for q in range(2):
             start = first_row + q * pitch[0] + QUARTER
             z_quarter = sums[:, start : start + HALF].bitcast(BF16)
-            rectify(slice(HALF + q * QUARTER, HALF + (q + 1) * QUARTER), z_quarter, on_vector=True)
+            rectify(quarters[2 + q], z_quarter, on_vector=True)
             z_last.append(z_quarter)
         last_quarters = [quantise_z(z_last[q], "quarter_%d" % q) for q in range(2)]
-        project_first_half(*first_half)
+        project_first_half(first_codes, first_scale)
         for q in range(2):
             project_quarter(q, *last_quarters[q])

@@ -19,9 +19,7 @@ P = 128
 PACK = 4
 HALF = S // 2
 QUARTER = S // 4
-EARLY = 2
 W1_SPLIT = 88
-LATE = 32
 
 
 def tile_picked_adain8_relu_p_kernel(tc, x_words, x_scales, w1, gamma, beta, w2, offs, sty, out):
@@ -30,18 +28,18 @@ def tile_picked_adain8_relu_p_kernel(tc, x_words, x_scales, w1, gamma, beta, w2,
         keep = ctx.enter_context(tc.tile_pool(name="keep", bufs=1))
         psum = ctx.enter_context(tc.psum_pool(name="psum", bufs=1))
 
+        def sb(name, cols, dtype):
+            return keep.tile([P, cols], dtype, name=name, align_bytes=64)
+
         offs_sb = keep.tile([P, S // 16], U16, name="offs_sb")
         sty_sb = keep.tile([P, S // 16], U16, name="sty_sb")
-        word_table = keep.tile([P, T], U32, name="word_table", align_bytes=64)
-        scale_table = keep.tile([P, T], U8, name="scale_table", align_bytes=64)
+        word_table = sb("word_table", T, U32)
+        scale_table = sb("scale_table", T, U8)
         w1_raw = keep.tile([P, PACK, H], F32, name="w1_raw", align_bytes=64)
-        w2_parts = (slice(0, N - LATE), slice(N - LATE, N))
-        reused = keep.tile([P, 3 * HALF], F32, name="reused", align_bytes=64)
-        w2_first = keep.tile([P, PACK, N - LATE], F32, name="w2_first", align_bytes=64)
-        w2_raw = [w2_first[:], reused[:].rearrange("p (j c) -> p j c", j=PACK)[:, :, :LATE]]
+        w2_raw = [keep.tile([P, PACK, N // 2], F32, name="w2_raw_%d" % g, align_bytes=64) for g in range(2)]
         w2_rows = w2.rearrange("(p j) c -> p j c", j=PACK)
-        gamma_sb = [keep.tile([P, U], F32, name="gamma_%d" % t, align_bytes=64) for t in range(PACK)]
-        beta_sb = [keep.tile([P, U], F32, name="beta_%d" % t, align_bytes=64) for t in range(PACK)]
+        gamma_sb = [sb("gamma_%d" % t, U, F32) for t in range(PACK)]
+        beta_sb = [sb("beta_%d" % t, U, F32) for t in range(PACK)]
         gamma_rows = gamma.rearrange("(p t) u -> p t u", t=PACK)
         beta_rows = beta.rearrange("(p t) u -> p t u", t=PACK)
 
@@ -59,223 +57,169 @@ def tile_picked_adain8_relu_p_kernel(tc, x_words, x_scales, w1, gamma, beta, w2,
         nc.sync.dma_start(w1_raw[:, 2:4, :], w1_rows[:, 2:4, :])
         nc.sync.dma_start(word_table[:].bitcast(I32), x_words[0].rearrange("p n t -> p (n t)").bitcast(I32))
         nc.sync.dma_start(sty_sb[:], sty)
-        for t in range(EARLY):
-            nc.sync.dma_start(beta_sb[t][:], beta_rows[:, t, :])
-        for t in range(EARLY):
+        for t in range(2):
             nc.sync.dma_start(gamma_sb[t][:], gamma_rows[:, t, :])
+            nc.sync.dma_start(beta_sb[t][:], beta_rows[:, t, :])
         nc.sync.dma_start(gamma_sb[2][:], gamma_rows[:, 2, :])
-        nc.sync.dma_start(w2_raw[0], w2_rows[:, :, w2_parts[0]])
         nc.sync.dma_start(gamma_sb[3][:], gamma_rows[:, 3, :])
         nc.sync.dma_start(beta_sb[2][:], beta_rows[:, 2, :])
         nc.sync.dma_start(beta_sb[3][:], beta_rows[:, 3, :])
-        nc.sync.dma_start(w2_raw[1], w2_rows[:, :, w2_parts[1]])
+        nc.sync.dma_start(w2_raw[0][:], w2_rows[:, :, 0 : N // 2])
+        nc.sync.dma_start(w2_raw[1][:], w2_rows[:, :, N // 2 : N])
 
-        x_scale = keep.tile([P, S], U8, name="x_scale", align_bytes=64)
+        x_scale = sb("x_scale", S, U8)
         nc.vector.tensor_copy(x_scale[:], scale_table[:].indirect(offs_sb[:]))
 
-        w1_bf16 = keep.tile([P, H * PACK], BF16, name="w1_bf16", align_bytes=64)
+        w1_bf16 = sb("w1_bf16", H * PACK, BF16)
         dst = w1_bf16[:].rearrange("p (t m j) -> p m j t", t=PACK, j=PACK)
         src = w1_raw[:].rearrange("p j (m t) -> p m j t", t=PACK)
         nc.vector.tensor_copy(dst[:, :W1_SPLIT], src[:, :W1_SPLIT])
         nc.scalar.copy(dst[:, W1_SPLIT:], src[:, W1_SPLIT:])
         w1_codes, w1_scale = [], []
         for u in range(2):
-            codes = keep.tile([P, 2 * P], U32, name="w1_codes_%d" % u, align_bytes=64)
-            scale = keep.tile([P, 2 * P], U8, name="w1_scale_%d" % u, align_bytes=64)
+            codes = sb("w1_codes_%d" % u, 2 * P, U32)
+            scale = sb("w1_scale_%d" % u, 2 * P, U8)
             nc.vector.quantize_mx(out=codes[:].bitcast(FP8X4), scales=scale[:], in_=w1_bf16[:, u * 2 * P * PACK : (u + 1) * 2 * P * PACK])
             w1_codes.append(codes)
             w1_scale.append(scale)
 
-        x_codes = keep.tile([P, S], U32, name="x_codes", align_bytes=64)
+        x_codes = sb("x_codes", S, U32)
         nc.vector.tensor_copy(x_codes[:], word_table[:].indirect(offs_sb[:]))
 
         y = [psum.tile([P, S], F32, name="y_%d" % t, tag="y_%d" % t) for t in range(PACK)]
-        folded = {t: psum.tile([P, P], F32, name="folded_%d" % t, tag="out_%d" % t) for t in range(EARLY, PACK)}
-
-        def first_product(t, target, places, start, stop):
+        for t in range(PACK):
             cols = slice((t % 2) * P, (t % 2 + 1) * P)
             nc.tensor.matmul_mx(
-                out=target,
+                out=y[t][:],
                 lhsT=w1_codes[t // 2][:, cols].bitcast(FP8X4),
                 lhsT_scale=w1_scale[t // 2][:, cols],
-                rhs=x_codes[:, places].bitcast(FP8X4),
-                rhs_scale=x_scale[:, places],
-                start=start,
-                stop=stop,
-            )
-
-        for t in range(EARLY):
-            first_product(t, y[t][:], slice(0, S), True, True)
-        for t in range(EARLY, PACK):
-            for c in range(PACK):
-                first_product(t, folded[t][:], slice(c * P, (c + 1) * P), c == 0, c == PACK - 1)
-            first_product(t, y[t][:], slice(0, S), True, True)
-
-        neg_mean, rstd = {}, {}
-        pitch = (S, 3 * S + QUARTER)
-        last_row = 3 * pitch[1]
-        first_row = last_row + QUARTER - 3 * pitch[0]
-        sums = keep.tile([P, PACK * pitch[1]], F32, name="sums", align_bytes=64)
-        pre = [
-            sums[:, start : start + PACK * pitch[a]].rearrange("p (t c) -> p t c", t=PACK)[:, :, :HALF]
-            for a, start in enumerate((first_row, 0))
-        ]
-        h = {(t, a): keep.tile([P, HALF], F32, name="h_%d_%d" % (t, a), align_bytes=64)[:] for t in range(EARLY, PACK) for a in range(2)}
-        centred = keep.tile([P, S], F32, name="centred", align_bytes=64)
-
-        def half(a):
-            return slice(a * HALF, (a + 1) * HALF)
-
-        def statistics(t):
-            small = keep.tile([P, 3], F32, name="small_%d" % t)
-            unused = keep.tile([P, S], BF16, name="unused_%d" % t, align_bytes=64)
-            mean_tile = keep.tile([P, 1], F32, name="mean_%d" % t, tag="w2_bf16" if t == 3 else "mean_%d" % t, align_bytes=64)
-            neg_mean[t], sum_sq, rstd[t], shift = mean_tile[:], small[:, 0:1], small[:, 1:2], small[:, 2:3]
-            if t < EARLY:
-                nc.scalar.activation(unused[:], y[t][:], ACT.Copy, scale=-1.0 / S, accum_out=neg_mean[t])
-            else:
-                nc.scalar.activation(unused[:, 0:P], folded[t][:], ACT.Copy, scale=-1.0 / S, accum_out=neg_mean[t])
-            nc.scalar.activation(unused[:], y[t][:], ACT.Square, bias=neg_mean[t], accum_out=sum_sq)
-            nc.scalar.activation(rstd[t], sum_sq, ACT.Abs_reciprocal_sqrt, scale=1.0 / S, bias=eps)
-            if t == 1:
-                nc.scalar.activation(centred[:], y[t][:], ACT.Identity, bias=neg_mean[t])
-            if t >= EARLY:
-                nc.scalar.activation(shift, rstd[t], ACT.Copy, scale=neg_mean[t])
-                for a in range(2):
-                    nc.scalar.activation(h[t, a], y[t][:, half(a)], ACT.Identity, scale=rstd[t], bias=shift)
-
-        scaled = {}
-
-        def styles(a):
-            return sty_sb[:, a * HALF // 16 : (a + 1) * HALF // 16]
-
-        picked_beta = [keep.tile([P, S], F32, name="picked_beta_%d" % t, align_bytes=64) for t in range(EARLY)]
-
-        def modulate_early(t):
-            for a in range(2):
-                scaled[t, a] = keep.tile([P, HALF], F32, name="scaled_%d_%d" % (t, a), align_bytes=64)
-            if t == 0:
-                picked_gamma = [keep.tile([P, HALF], F32, name="picked_gamma_%d" % a, align_bytes=64) for a in range(2)]
-                for a in range(2):
-                    nc.vector.tensor_copy(picked_gamma[a][:], gamma_sb[t][:].indirect(styles(a)))
-                for a in range(2):
-                    nc.vector.scalar_tensor_tensor(scaled[t, a][:], y[t][:, half(a)], neg_mean[t], picked_gamma[a][:], ALU.add, ALU.mult)
-            else:
-                for a in range(2):
-                    nc.vector.tensor_tensor(scaled[t, a][:], gamma_sb[t][:].indirect(styles(a)), centred[:, half(a)], ALU.mult)
-            for a in range(2):
-                nc.vector.scalar_tensor_tensor(pre[a][:, t, :], scaled[t, a][:], rstd[t], picked_beta[t][:, half(a)], ALU.mult, ALU.add)
-
-        def scale_late(t, a):
-            if (t, a) == (3, 1):
-                scaled[t, a] = reused[:, :HALF]
-            else:
-                scaled[t, a] = keep.tile([P, HALF], F32, name="scaled_%d_%d" % (t, a), align_bytes=64)[:]
-            nc.vector.tensor_tensor(scaled[t, a], gamma_sb[t][:].indirect(styles(a)), h[t, a], ALU.mult)
-
-        def shift_late(t, a):
-            nc.vector.tensor_tensor(pre[a][:, t, :], beta_sb[t][:].indirect(styles(a)), scaled[t, a], ALU.add)
-
-        w2_codes = keep.tile([P, N], U32, name="w2_codes", align_bytes=64)
-        w2_scale = keep.tile([P, N], U8, name="w2_scale", align_bytes=64)
-
-        def cast_w2():
-            for g, c in enumerate(w2_parts):
-                dst = w2_bf16[:, PACK * c.start : PACK * c.stop].rearrange("p (c i j) -> p c j i", i=4, j=PACK)
-                src = w2_raw[g].rearrange("p j (c i) -> p c j i", i=4)
-                nc.scalar.copy(dst, src)
-
-        def rectify(places, z_bf16, on_vector):
-            a, first, count = places.start // HALF, places.start % HALF, places.stop - places.start
-            dst = z_bf16.rearrange("p (c i t) -> p c t i", i=4, t=PACK)
-            src = pre[a][:, 0:PACK, first : first + count].rearrange("p t (c i) -> p c t i", i=4)
-            if on_vector:
-                nc.vector.tensor_scalar(dst, src, 0.0, None, ALU.max)
-            else:
-                nc.scalar.activation(dst, src, ACT.Relu)
-
-        def quantise_z(z_bf16, label):
-            count = z_bf16.shape[1] // PACK
-            codes = keep.tile([P, count], U32, name="z_codes_" + label, align_bytes=64)
-            scale = keep.tile([P, count], U8, name="z_scale_" + label, align_bytes=64)
-            nc.vector.quantize_mx(out=codes[:].bitcast(FP8X4), scales=scale[:], in_=z_bf16)
-            return codes, scale
-
-        def second_product(target, m, codes, scale):
-            cols = slice(m * P, (m + 1) * P)
-            nc.tensor.matmul_mx(
-                out=target,
-                lhsT=w2_codes[:, cols].bitcast(FP8X4),
-                lhsT_scale=w2_scale[:, cols],
-                rhs=codes.bitcast(FP8X4),
-                rhs_scale=scale,
+                rhs=x_codes[:].bitcast(FP8X4),
+                rhs_scale=x_scale[:],
                 start=True,
                 stop=True,
             )
 
-        def project_first_half(codes, scale):
-            banks = [psum.tile([P, HALF], F32, name="o_%d" % m, tag="out_%d" % m) for m in range(PACK)]
-            for q in range(2):
-                places = slice(q * QUARTER, (q + 1) * QUARTER)
-                for m in range(PACK):
-                    second_product(banks[m][:, places], m, codes[:, places], scale[:, places])
-            for m, bank in enumerate(banks):
-                staged = keep.tile([P, HALF], F32, name="staged_%d" % m, align_bytes=64)
-                nc.scalar.copy(staged[:], bank[:])
-                nc.sync.dma_start(out[m * P : (m + 1) * P, half(0)], staged[:])
+        def half(a):
+            return slice(a * HALF, (a + 1) * HALF)
 
-        def project_quarter(q, codes, scale):
-            places = slice(HALF + q * QUARTER, HALF + (q + 1) * QUARTER)
-            for g in range(2):
-                bank = psum.tile([P, 2, QUARTER], F32, name="o_%d_%d" % (q, g), tag="y_%d" % (2 * q + g))
-                for i in range(2):
-                    second_product(bank[:, i, :], 2 * g + i, codes[:], scale[:])
-                staged = keep.tile([P, 2, QUARTER], F32, name="staged_%d_%d" % (q, g), align_bytes=64)
-                if g == 0:
-                    nc.scalar.copy(staged[:], bank[:])
-                else:
-                    nc.vector.tensor_copy(staged[:], bank[:])
-                rows = out[2 * g * P : 2 * (g + 1) * P, places]
-                nc.sync.dma_start(rows.rearrange("(i p) c -> p i c", p=P), staged[:])
+        def styles(a):
+            return sty_sb[:, a * HALF // 16 : (a + 1) * HALF // 16]
 
-        for t in range(PACK):
-            statistics(t)
-        for t in range(EARLY):
-            nc.vector.tensor_copy(picked_beta[t][:], beta_sb[t][:].indirect(sty_sb[:]))
-        for t in range(EARLY):
-            modulate_early(t)
-        w2_bf16 = keep.tile([P, N * PACK], BF16, name="w2_bf16", tag="w2_bf16", align_bytes=64)
-        scale_late(2, 0)
-        scale_late(2, 1)
-        scale_late(3, 0)
-        shift_late(2, 0)
-        shift_late(2, 1)
-        shift_late(3, 0)
-        cast_w2()
-        nc.vector.quantize_mx(out=w2_codes[:].bitcast(FP8X4), scales=w2_scale[:], in_=w2_bf16[:])
-        scale_late(3, 1)
-        z_first = reused[:, HALF:].bitcast(BF16)
-        first_codes = keep.tile([P, HALF], U32, name="z_codes_first", align_bytes=64)
-        first_scale = keep.tile([P, HALF], U8, name="z_scale_first", align_bytes=64)
-        quarters = [slice(q * QUARTER, (q + 1) * QUARTER) for q in range(PACK)]
+        picked_gamma = [sb("picked_gamma_%d" % t, S, F32) for t in range(3)]
+        picked_beta = [sb("picked_beta_%d" % t, S, F32) for t in range(3)]
+        nc.scalar.activation(picked_gamma[0][:, half(0)], gamma_sb[0][:].indirect(styles(0)), ACT.Copy)
+        nc.vector.tensor_copy(picked_gamma[0][:, half(1)], gamma_sb[0][:].indirect(styles(1)))
 
-        def quantise_first(q):
-            places = quarters[q]
-            z_bf16 = z_first[:, PACK * places.start : PACK * places.stop]
-            nc.vector.quantize_mx(out=first_codes[:, places].bitcast(FP8X4), scales=first_scale[:, places], in_=z_bf16)
+        moments = keep.tile([P, PACK, 2], F32, name="moments")
+        stats_all = keep.tile([P, PACK, 8], F32, name="stats_all", tag="gamma_0", align_bytes=64)
+        stats = [stats_all[:, t, 0:6] for t in range(PACK)]
+        for t in range(PACK + 1):
+            if t < PACK:
+                nc.vector.bn_stats(stats[t], y[t][:])
+            if t > 0:
+                nc.vector.bn_aggr(moments[:, t - 1, :], stats[t - 1])
 
-        for places in quarters[:2]:
-            rectify(places, z_first[:, PACK * places.start : PACK * places.stop], on_vector=False)
-        quantise_first(0)
-        shift_late(3, 1)
-        quantise_first(1)
-        z_last = []
-        for q in range(2):
-            start = first_row + q * pitch[0] + QUARTER
-            z_quarter = sums[:, start : start + HALF].bitcast(BF16)
-            rectify(quarters[2 + q], z_quarter, on_vector=True)
-            z_last.append(z_quarter)
-        last_quarters = [quantise_z(z_last[q], "quarter_%d" % q) for q in range(2)]
-        project_first_half(first_codes, first_scale)
-        for q in range(2):
-            project_quarter(q, *last_quarters[q])
+        nc.scalar.activation(picked_beta[0][:], beta_sb[0][:].indirect(sty_sb[:]), ACT.Copy)
+        for t in (1, 2):
+            nc.scalar.activation(picked_gamma[t][:], gamma_sb[t][:].indirect(sty_sb[:]), ACT.Copy)
+            if t == 1:
+                rstd = keep.tile([P, PACK], F32, name="rstd", tag="gamma_1", align_bytes=64)
+                nc.scalar.activation(rstd[:], moments[:, :, 1], ACT.Abs_reciprocal_sqrt, bias=eps)
+            if t == 2:
+                for a in range(2):
+                    nc.scalar.activation(picked_beta[t][:, half(a)], beta_sb[t][:].indirect(styles(a)), ACT.Copy)
+            else:
+                nc.scalar.activation(picked_beta[t][:], beta_sb[t][:].indirect(sty_sb[:]), ACT.Copy)
+            if t == 1:
+                offset = keep.tile([P, 1], F32, name="offset")
+                nc.gpsimd.tensor_scalar(offset[:], moments[:, 3, 0:1], rstd[:, 3:4], -1.0, ALU.mult, ALU.mult)
+                normal = keep.tile([P, S], F32, name="normal", tag="beta_1", align_bytes=64)
+                nc.scalar.activation(normal[:], y[3][:], ACT.Identity, scale=rstd[:, 3:4], bias=offset[:])
+
+        scaled_all = keep.tile([P, 2, S], F32, name="scaled_all", tag="gamma_0", align_bytes=64)
+        scaled = [scaled_all[:, 0, :], scaled_all[:, 1, :], normal[:]]
+
+        pre = keep.tile([P, PACK, S], F32, name="pre", align_bytes=64)
+        scaled_last = [pre[:, 2, half(1)], sb("scaled_last_1", HALF, F32)[:]]
+
+        def centre(t, places):
+            nc.vector.scalar_tensor_tensor(scaled[t][:, places], y[t][:, places], moments[:, t, 0:1], picked_gamma[t][:, places], ALU.subtract, ALU.mult)
+
+        def shift(t, places):
+            nc.vector.scalar_tensor_tensor(pre[:, t, places], scaled[t][:, places], rstd[:, t : t + 1], picked_beta[t][:, places], ALU.mult, ALU.add)
+
+        w2_bf16 = [sb("w2_bf16_%d" % g, N // 2 * PACK, BF16) for g in range(2)]
+        w2_codes = {}
+        w2_scale = [sb("w2_scale_%d" % g, N // 2, U8) for g in range(2)]
+
+        def cast_w2(g, groups, engine_copy):
+            dst = w2_bf16[g][:].rearrange("p (c i j) -> p c j i", i=4, j=PACK)
+            src = w2_raw[g][:].rearrange("p j (c i) -> p c j i", i=4)
+            engine_copy(dst[:, groups], src[:, groups])
+
+        def quantise_w2(g):
+            w2_codes[g] = sb("w2_codes_%d" % g, N // 2, U32)
+            nc.vector.quantize_mx(out=w2_codes[g][:].bitcast(FP8X4), scales=w2_scale[g][:], in_=w2_bf16[g][:])
+
+        z_bf16 = [sb("z_bf16_%d" % a, HALF * PACK, BF16) for a in range(2)]
+        z_codes = [sb("z_codes_%d" % a, HALF, U32) for a in range(2)]
+        z_scale = [sb("z_scale_%d" % a, HALF, U8) for a in range(2)]
+
+        def rectify(q):
+            dst = z_bf16[q // 2][:, (q % 2) * QUARTER * PACK : (q % 2 + 1) * QUARTER * PACK].rearrange("p (c i t) -> p c t i", i=4, t=PACK)
+            src = pre[:, :, q * QUARTER : (q + 1) * QUARTER].rearrange("p t (c i) -> p c t i", i=4)
+            nc.scalar.activation(dst, src, ACT.Relu)
+
+        def scale_last(a):
+            nc.vector.tensor_tensor(scaled_last[a], gamma_sb[3][:].indirect(styles(a)), normal[:, half(a)], ALU.mult)
+
+        def shift_last(a):
+            nc.vector.tensor_tensor(pre[:, 3, half(a)], beta_sb[3][:].indirect(styles(a)), scaled_last[a], ALU.add)
+
+        def quantise_z(a):
+            nc.vector.quantize_mx(out=z_codes[a][:].bitcast(FP8X4), scales=z_scale[a][:], in_=z_bf16[a][:])
+
+        def project(m, a, tag, engine_copy):
+            cols = slice((m % 2) * P, (m % 2 + 1) * P)
+            bank = psum.tile([P, HALF], F32, name="o_%d_%d" % (m, a), tag=tag)
+            nc.tensor.matmul_mx(
+                out=bank[:],
+                lhsT=w2_codes[m // 2][:, cols].bitcast(FP8X4),
+                lhsT_scale=w2_scale[m // 2][:, cols],
+                rhs=z_codes[a][:].bitcast(FP8X4),
+                rhs_scale=z_scale[a][:],
+                start=True,
+                stop=True,
+            )
+            staged = sb("staged_%d_%d" % (m, a), HALF, F32)
+            engine_copy(staged[:], bank[:])
+            nc.sync.dma_start(out[m * P : (m + 1) * P, half(a)], staged[:])
+
+        whole = slice(0, S)
+        centre(0, whole)
+        centre(1, whole)
+        shift(0, whole)
+        shift(1, whole)
+        scale_last(0)
+        scale_last(1)
+        centre(2, half(0))
+        centre(2, half(1))
+        shift(2, half(0))
+        shift_last(0)
+        shift(2, half(1))
+        picked_last = sb("picked_last", HALF, F32)
+        nc.scalar.activation(picked_last[:], beta_sb[3][:].indirect(styles(1)), ACT.Copy)
+        nc.vector.tensor_tensor(pre[:, 3, half(1)], scaled_last[1], picked_last[:], ALU.add)
+        for q in range(4):
+            rectify(q)
+        cast_w2(0, slice(0, 64), nc.vector.tensor_copy)
+        quantise_z(0)
+        quantise_w2(0)
+        cast_w2(1, slice(0, 40), nc.vector.tensor_copy)
+        cast_w2(1, slice(40, 64), nc.scalar.copy)
+        quantise_z(1)
+        quantise_w2(1)
+        for m, a in ((0, 0), (1, 0), (0, 1), (1, 1)):
+            project(m, a, "out_%d" % (2 * a + m), nc.scalar.copy)
+        for m, a in ((2, 0), (3, 0), (2, 1), (3, 1)):
+            project(m, a, "y_%d" % (2 * a + m - 2), nc.vector.tensor_copy if m == 2 else nc.scalar.copy)

@@ -36,7 +36,7 @@ def tile_picked_adain8_relu_p_kernel(tc, x_words, x_scales, w1, gamma, beta, w2,
         word_table = sb("word_table", T, U32)
         scale_table = sb("scale_table", T, U8)
         w1_raw = keep.tile([P, PACK, H], F32, name="w1_raw", align_bytes=64)
-        w2_raw = [keep.tile([P, PACK, N // 2], F32, name="w2_raw_%d" % g, align_bytes=64) for g in range(2)]
+        w2_raw = [keep.tile([P, PACK, P], F32, name="w2_raw_%d" % g, align_bytes=64) for g in range(PACK)]
         w2_rows = w2.rearrange("(p j) c -> p j c", j=PACK)
         gamma_sb = [sb("gamma_%d" % t, U, F32) for t in range(PACK)]
         beta_sb = [sb("beta_%d" % t, U, F32) for t in range(PACK)]
@@ -64,8 +64,8 @@ def tile_picked_adain8_relu_p_kernel(tc, x_words, x_scales, w1, gamma, beta, w2,
         nc.sync.dma_start(gamma_sb[3][:], gamma_rows[:, 3, :])
         nc.sync.dma_start(beta_sb[2][:], beta_rows[:, 2, :])
         nc.sync.dma_start(beta_sb[3][:], beta_rows[:, 3, :])
-        nc.sync.dma_start(w2_raw[0][:], w2_rows[:, :, 0 : N // 2])
-        nc.sync.dma_start(w2_raw[1][:], w2_rows[:, :, N // 2 : N])
+        for g in range(PACK):
+            nc.sync.dma_start(w2_raw[g][:], w2_rows[:, :, g * P : (g + 1) * P])
 
         x_scale = sb("x_scale", S, U8)
         nc.vector.tensor_copy(x_scale[:], scale_table[:].indirect(offs_sb[:]))
@@ -148,9 +148,9 @@ def tile_picked_adain8_relu_p_kernel(tc, x_words, x_scales, w1, gamma, beta, w2,
         def shift(t, places):
             nc.vector.scalar_tensor_tensor(pre[:, t, places], scaled[t][:, places], rstd[:, t : t + 1], picked_beta[t][:, places], ALU.mult, ALU.add)
 
-        w2_bf16 = [sb("w2_bf16_%d" % g, N // 2 * PACK, BF16) for g in range(2)]
+        w2_bf16 = [sb("w2_bf16_%d" % g, P * PACK, BF16) for g in range(PACK)]
         w2_codes = {}
-        w2_scale = [sb("w2_scale_%d" % g, N // 2, U8) for g in range(2)]
+        w2_scale = [sb("w2_scale_%d" % g, P, U8) for g in range(PACK)]
 
         def cast_w2(g, groups, engine_copy):
             dst = w2_bf16[g][:].rearrange("p (c i j) -> p c j i", i=4, j=PACK)
@@ -158,17 +158,20 @@ def tile_picked_adain8_relu_p_kernel(tc, x_words, x_scales, w1, gamma, beta, w2,
             engine_copy(dst[:, groups], src[:, groups])
 
         def quantise_w2(g):
-            w2_codes[g] = sb("w2_codes_%d" % g, N // 2, U32)
+            w2_codes[g] = sb("w2_codes_%d" % g, P, U32)
             nc.vector.quantize_mx(out=w2_codes[g][:].bitcast(FP8X4), scales=w2_scale[g][:], in_=w2_bf16[g][:])
 
         z_bf16 = [sb("z_bf16_%d" % a, HALF * PACK, BF16) for a in range(2)]
         z_codes = [sb("z_codes_%d" % a, HALF, U32) for a in range(2)]
         z_scale = [sb("z_scale_%d" % a, HALF, U8) for a in range(2)]
 
-        def rectify(q):
+        def rectify(q, on_vector):
             dst = z_bf16[q // 2][:, (q % 2) * QUARTER * PACK : (q % 2 + 1) * QUARTER * PACK].rearrange("p (c i t) -> p c t i", i=4, t=PACK)
             src = pre[:, :, q * QUARTER : (q + 1) * QUARTER].rearrange("p t (c i) -> p c t i", i=4)
-            nc.scalar.activation(dst, src, ACT.Relu)
+            if on_vector:
+                nc.vector.tensor_scalar(dst, src, 0.0, None, ALU.max)
+            else:
+                nc.scalar.activation(dst, src, ACT.Relu)
 
         def scale_last(a):
             nc.vector.tensor_tensor(scaled_last[a], gamma_sb[3][:].indirect(styles(a)), normal[:, half(a)], ALU.mult)
@@ -180,12 +183,11 @@ def tile_picked_adain8_relu_p_kernel(tc, x_words, x_scales, w1, gamma, beta, w2,
             nc.vector.quantize_mx(out=z_codes[a][:].bitcast(FP8X4), scales=z_scale[a][:], in_=z_bf16[a][:])
 
         def project(m, a, tag, engine_copy):
-            cols = slice((m % 2) * P, (m % 2 + 1) * P)
             bank = psum.tile([P, HALF], F32, name="o_%d_%d" % (m, a), tag=tag)
             nc.tensor.matmul_mx(
                 out=bank[:],
-                lhsT=w2_codes[m // 2][:, cols].bitcast(FP8X4),
-                lhsT_scale=w2_scale[m // 2][:, cols],
+                lhsT=w2_codes[m][:].bitcast(FP8X4),
+                lhsT_scale=w2_scale[m][:],
                 rhs=z_codes[a][:].bitcast(FP8X4),
                 rhs_scale=z_scale[a][:],
                 start=True,
@@ -210,16 +212,22 @@ def tile_picked_adain8_relu_p_kernel(tc, x_words, x_scales, w1, gamma, beta, w2,
         picked_last = sb("picked_last", HALF, F32)
         nc.scalar.activation(picked_last[:], beta_sb[3][:].indirect(styles(1)), ACT.Copy)
         nc.vector.tensor_tensor(pre[:, 3, half(1)], scaled_last[1], picked_last[:], ALU.add)
-        for q in range(4):
-            rectify(q)
-        cast_w2(0, slice(0, 64), nc.vector.tensor_copy)
+        every = slice(0, P // 4)
+        rectify(0, False)
+        rectify(1, True)
+        rectify(2, False)
+        cast_w2(0, every, nc.vector.tensor_copy)
         quantise_z(0)
         quantise_w2(0)
-        cast_w2(1, slice(0, 40), nc.vector.tensor_copy)
-        cast_w2(1, slice(40, 64), nc.scalar.copy)
-        quantise_z(1)
+        cast_w2(1, every, nc.scalar.copy)
+        cast_w2(2, every, nc.scalar.copy)
+        rectify(3, True)
         quantise_w2(1)
+        quantise_z(1)
+        quantise_w2(2)
+        cast_w2(3, every, nc.vector.tensor_copy)
+        quantise_w2(3)
         for m, a in ((0, 0), (1, 0), (0, 1), (1, 1)):
             project(m, a, "out_%d" % (2 * a + m), nc.scalar.copy)
-        for m, a in ((2, 0), (3, 0), (2, 1), (3, 1)):
-            project(m, a, "y_%d" % (2 * a + m - 2), nc.vector.tensor_copy if m == 2 else nc.scalar.copy)
+        for m, a in ((2, 0), (2, 1), (3, 0), (3, 1)):
+            project(m, a, "y_%d" % (2 * (m - 2) + a), nc.vector.tensor_copy if a == 0 else nc.scalar.copy)

@@ -19,7 +19,8 @@ P = 128
 PACK = 4
 HALF = S // 2
 QUARTER = S // 4
-W1_SPLIT = 88
+W1_HALF = H // 2
+W1_VECTOR = (42, 42)
 
 
 def tile_picked_adain8_relu_p_kernel(tc, x_words, x_scales, w1, gamma, beta, w2, offs, sty, out):
@@ -28,20 +29,27 @@ def tile_picked_adain8_relu_p_kernel(tc, x_words, x_scales, w1, gamma, beta, w2,
         keep = ctx.enter_context(tc.tile_pool(name="keep", bufs=1))
         psum = ctx.enter_context(tc.psum_pool(name="psum", bufs=1))
 
-        def sb(name, cols, dtype):
-            return keep.tile([P, cols], dtype, name=name, align_bytes=64)
+        def sb(name, cols, dtype, tag=None):
+            return keep.tile([P, cols], dtype, name=name, tag=tag or name, align_bytes=64)
+
+        def half(a):
+            return slice(a * HALF, (a + 1) * HALF)
 
         offs_sb = keep.tile([P, S // 16], U16, name="offs_sb")
         sty_sb = keep.tile([P, S // 16], U16, name="sty_sb")
         word_table = sb("word_table", T, U32)
         scale_table = sb("scale_table", T, U8)
-        w1_raw = keep.tile([P, PACK, H], F32, name="w1_raw", align_bytes=64)
+        w1_raw = [keep.tile([P, PACK, W1_HALF], F32, name="w1_raw_%d" % u, align_bytes=64) for u in range(2)]
         w2_raw = [keep.tile([P, PACK, P], F32, name="w2_raw_%d" % g, align_bytes=64) for g in range(PACK)]
-        w2_rows = w2.rearrange("(p j) c -> p j c", j=PACK)
         gamma_sb = [sb("gamma_%d" % t, U, F32) for t in range(PACK)]
         beta_sb = [sb("beta_%d" % t, U, F32) for t in range(PACK)]
+        w1_rows = w1.rearrange("(p j) c -> p j c", j=PACK)
+        w2_rows = w2.rearrange("(p j) c -> p j c", j=PACK)
         gamma_rows = gamma.rearrange("(p t) u -> p t u", t=PACK)
         beta_rows = beta.rearrange("(p t) u -> p t u", t=PACK)
+
+        def styles(a):
+            return sty_sb[:, a * HALF // 16 : (a + 1) * HALF // 16]
 
         nc.vector.memset(scale_table[:].bitcast(I32), 0)
         consts = keep.tile([P, 2], F32, name="consts")
@@ -49,98 +57,75 @@ def tile_picked_adain8_relu_p_kernel(tc, x_words, x_scales, w1, gamma, beta, w2,
         nc.vector.memset(one, 1.0)
         nc.scalar.activation(eps, one, ACT.Abs_reciprocal_sqrt, scale=1e10)
 
-        w1_rows = w1.rearrange("(p j) c -> p j c", j=PACK)
-        nc.sync.dma_start(w1_raw[:, 0:2, :], w1_rows[:, 0:2, :])
+        nc.sync.dma_start(w1_raw[0][:], w1_rows[:, :, :W1_HALF])
         for r in range(4):
             nc.sync.dma_start(scale_table[r:P:32, :].bitcast(I32), x_scales[0, r:16:4, :].bitcast(I32))
         nc.sync.dma_start(offs_sb[:], offs)
-        nc.sync.dma_start(w1_raw[:, 2:4, :], w1_rows[:, 2:4, :])
         nc.sync.dma_start(word_table[:].bitcast(I32), x_words[0].rearrange("p n t -> p (n t)").bitcast(I32))
+        nc.sync.dma_start(w1_raw[1][:], w1_rows[:, :, W1_HALF:])
         nc.sync.dma_start(sty_sb[:], sty)
         for t in range(2):
             nc.sync.dma_start(gamma_sb[t][:], gamma_rows[:, t, :])
             nc.sync.dma_start(beta_sb[t][:], beta_rows[:, t, :])
-        nc.sync.dma_start(gamma_sb[2][:], gamma_rows[:, 2, :])
-        nc.sync.dma_start(gamma_sb[3][:], gamma_rows[:, 3, :])
-        nc.sync.dma_start(beta_sb[2][:], beta_rows[:, 2, :])
-        nc.sync.dma_start(beta_sb[3][:], beta_rows[:, 3, :])
+        for t in (2, 3):
+            nc.sync.dma_start(gamma_sb[t][:], gamma_rows[:, t, :])
+        for t in (2, 3):
+            nc.sync.dma_start(beta_sb[t][:], beta_rows[:, t, :])
         for g in range(PACK):
             nc.sync.dma_start(w2_raw[g][:], w2_rows[:, :, g * P : (g + 1) * P])
 
+        x_codes = sb("x_codes", S, U32)
         x_scale = sb("x_scale", S, U8)
         nc.vector.tensor_copy(x_scale[:], scale_table[:].indirect(offs_sb[:]))
-
-        w1_bf16 = sb("w1_bf16", H * PACK, BF16)
-        dst = w1_bf16[:].rearrange("p (t m j) -> p m j t", t=PACK, j=PACK)
-        src = w1_raw[:].rearrange("p j (m t) -> p m j t", t=PACK)
-        nc.vector.tensor_copy(dst[:, :W1_SPLIT], src[:, :W1_SPLIT])
-        nc.scalar.copy(dst[:, W1_SPLIT:], src[:, W1_SPLIT:])
-        w1_codes, w1_scale = [], []
-        for u in range(2):
-            codes = sb("w1_codes_%d" % u, 2 * P, U32)
-            scale = sb("w1_scale_%d" % u, 2 * P, U8)
-            nc.vector.quantize_mx(out=codes[:].bitcast(FP8X4), scales=scale[:], in_=w1_bf16[:, u * 2 * P * PACK : (u + 1) * 2 * P * PACK])
-            w1_codes.append(codes)
-            w1_scale.append(scale)
-
-        x_codes = sb("x_codes", S, U32)
         nc.vector.tensor_copy(x_codes[:], word_table[:].indirect(offs_sb[:]))
+
+        w1_codes = [sb("w1_codes_%d" % t, P, U32) for t in range(PACK)]
+        w1_scale = [sb("w1_scale_%d" % t, P, U8) for t in range(PACK)]
+        for u in range(2):
+            w1_bf16 = sb("w1_bf16_%d" % u, W1_HALF * PACK, BF16)
+            dst = w1_bf16[:].rearrange("p (t m j) -> p m j t", t=PACK, j=PACK)
+            src = w1_raw[u][:].rearrange("p j (m t) -> p m j t", t=PACK)
+            nc.scalar.copy(dst[:, W1_VECTOR[u] :], src[:, W1_VECTOR[u] :])
+            nc.vector.tensor_copy(dst[:, : W1_VECTOR[u]], src[:, : W1_VECTOR[u]])
+            cols = slice(u * P // 2, (u + 1) * P // 2)
+            for t in range(PACK):
+                nc.vector.quantize_mx(out=w1_codes[t][:, cols].bitcast(FP8X4), scales=w1_scale[t][:, cols], in_=w1_bf16[:, t * W1_HALF : (t + 1) * W1_HALF])
 
         y = [psum.tile([P, S], F32, name="y_%d" % t, tag="y_%d" % t) for t in range(PACK)]
         for t in range(PACK):
-            cols = slice((t % 2) * P, (t % 2 + 1) * P)
             nc.tensor.matmul_mx(
                 out=y[t][:],
-                lhsT=w1_codes[t // 2][:, cols].bitcast(FP8X4),
-                lhsT_scale=w1_scale[t // 2][:, cols],
+                lhsT=w1_codes[t][:].bitcast(FP8X4),
+                lhsT_scale=w1_scale[t][:],
                 rhs=x_codes[:].bitcast(FP8X4),
                 rhs_scale=x_scale[:],
                 start=True,
                 stop=True,
             )
 
-        def half(a):
-            return slice(a * HALF, (a + 1) * HALF)
-
-        def styles(a):
-            return sty_sb[:, a * HALF // 16 : (a + 1) * HALF // 16]
+        stats = keep.tile([P, PACK, 8], F32, name="stats")
+        for t in range(PACK):
+            nc.vector.bn_stats(stats[:, t, 0:6], y[t][:])
+        moments = keep.tile([P, PACK, 2], F32, name="moments", tag="w1_codes_3", align_bytes=64)
+        for t in range(PACK):
+            nc.vector.bn_aggr(moments[:, t, :], stats[:, t, 0:6])
 
         picked_gamma = [sb("picked_gamma_%d" % t, S, F32) for t in range(3)]
         picked_beta = [sb("picked_beta_%d" % t, S, F32) for t in range(3)]
-        nc.scalar.activation(picked_gamma[0][:, half(0)], gamma_sb[0][:].indirect(styles(0)), ACT.Copy)
-        nc.vector.tensor_copy(picked_gamma[0][:, half(1)], gamma_sb[0][:].indirect(styles(1)))
+        late_beta = sb("late_beta", HALF, F32)
 
-        moments = keep.tile([P, PACK, 2], F32, name="moments")
-        stats_all = keep.tile([P, PACK, 8], F32, name="stats_all", tag="gamma_0", align_bytes=64)
-        stats = [stats_all[:, t, 0:6] for t in range(PACK)]
-        for t in range(PACK + 1):
-            if t < PACK:
-                nc.vector.bn_stats(stats[t], y[t][:])
-            if t > 0:
-                nc.vector.bn_aggr(moments[:, t - 1, :], stats[t - 1])
+        def pick(dst, table, offsets):
+            nc.scalar.activation(dst, table[:].indirect(offsets), ACT.Copy)
 
-        nc.scalar.activation(picked_beta[0][:], beta_sb[0][:].indirect(sty_sb[:]), ACT.Copy)
-        for t in (1, 2):
-            nc.scalar.activation(picked_gamma[t][:], gamma_sb[t][:].indirect(sty_sb[:]), ACT.Copy)
-            if t == 1:
-                rstd = keep.tile([P, PACK], F32, name="rstd", tag="gamma_1", align_bytes=64)
-                nc.scalar.activation(rstd[:], moments[:, :, 1], ACT.Abs_reciprocal_sqrt, bias=eps)
-            if t == 2:
-                for a in range(2):
-                    nc.scalar.activation(picked_beta[t][:, half(a)], beta_sb[t][:].indirect(styles(a)), ACT.Copy)
-            else:
-                nc.scalar.activation(picked_beta[t][:], beta_sb[t][:].indirect(sty_sb[:]), ACT.Copy)
-            if t == 1:
-                offset = keep.tile([P, 1], F32, name="offset")
-                nc.gpsimd.tensor_scalar(offset[:], moments[:, 3, 0:1], rstd[:, 3:4], -1.0, ALU.mult, ALU.mult)
-                normal = keep.tile([P, S], F32, name="normal", tag="beta_1", align_bytes=64)
-                nc.scalar.activation(normal[:], y[3][:], ACT.Identity, scale=rstd[:, 3:4], bias=offset[:])
-
-        scaled_all = keep.tile([P, 2, S], F32, name="scaled_all", tag="gamma_0", align_bytes=64)
-        scaled = [scaled_all[:, 0, :], scaled_all[:, 1, :], normal[:]]
-
+        pick(picked_gamma[0][:], gamma_sb[0], sty_sb[:])
+        pick(picked_beta[0][:], beta_sb[0], sty_sb[:])
+        pick(picked_gamma[1][:], gamma_sb[1], sty_sb[:])
+        rstd = sb("rstd", PACK, F32, tag="gamma_1")
+        nc.scalar.activation(rstd[:], moments[:, :, 1], ACT.Abs_reciprocal_sqrt, bias=eps)
+        pick(picked_beta[1][:], beta_sb[1], sty_sb[:])
+        normal = sb("normal", S, F32)
+        scaled = [sb("scaled_0", S, F32), sb("scaled_1", S, F32), normal, sb("scaled_3", S, F32)]
         pre = keep.tile([P, PACK, S], F32, name="pre", align_bytes=64)
-        scaled_last = [pre[:, 2, half(1)], sb("scaled_last_1", HALF, F32)[:]]
 
         def centre(t, places):
             nc.vector.scalar_tensor_tensor(scaled[t][:, places], y[t][:, places], moments[:, t, 0:1], picked_gamma[t][:, places], ALU.subtract, ALU.mult)
@@ -148,22 +133,40 @@ def tile_picked_adain8_relu_p_kernel(tc, x_words, x_scales, w1, gamma, beta, w2,
         def shift(t, places):
             nc.vector.scalar_tensor_tensor(pre[:, t, places], scaled[t][:, places], rstd[:, t : t + 1], picked_beta[t][:, places], ALU.mult, ALU.add)
 
+        whole = slice(0, S)
+        centre(0, whole)
+        centre(1, whole)
+        shift(0, whole)
+        nc.vector.tensor_scalar(normal[:], y[3][:], moments[:, 3, 0:1], rstd[:, 3:4], ALU.subtract, ALU.mult)
+        shift(1, whole)
+
+        pick(picked_gamma[2][:], gamma_sb[2], sty_sb[:])
+        for a in range(2):
+            pick(picked_beta[2][:, half(a)], beta_sb[2], styles(a))
+        for a in range(2):
+            nc.vector.tensor_tensor(scaled[3][:, half(a)], gamma_sb[3][:].indirect(styles(a)), normal[:, half(a)], ALU.mult)
+        centre(2, half(0))
+        centre(2, half(1))
+        shift(2, half(0))
+        shift(2, half(1))
+        pick(late_beta[:], beta_sb[3], styles(1))
+        nc.vector.tensor_tensor(pre[:, 3, half(0)], beta_sb[3][:].indirect(styles(0)), scaled[3][:, half(0)], ALU.add)
+        nc.vector.tensor_tensor(pre[:, 3, half(1)], late_beta[:], scaled[3][:, half(1)], ALU.add)
+
         w2_bf16 = [sb("w2_bf16_%d" % g, P * PACK, BF16) for g in range(PACK)]
-        w2_codes = {}
+        w2_codes = [sb("w2_codes_%d" % g, P, U32) for g in range(PACK)]
         w2_scale = [sb("w2_scale_%d" % g, P, U8) for g in range(PACK)]
-
-        def cast_w2(g, groups, engine_copy):
-            dst = w2_bf16[g][:].rearrange("p (c i j) -> p c j i", i=4, j=PACK)
-            src = w2_raw[g][:].rearrange("p j (c i) -> p c j i", i=4)
-            engine_copy(dst[:, groups], src[:, groups])
-
-        def quantise_w2(g):
-            w2_codes[g] = sb("w2_codes_%d" % g, P, U32)
-            nc.vector.quantize_mx(out=w2_codes[g][:].bitcast(FP8X4), scales=w2_scale[g][:], in_=w2_bf16[g][:])
-
         z_bf16 = [sb("z_bf16_%d" % a, HALF * PACK, BF16) for a in range(2)]
         z_codes = [sb("z_codes_%d" % a, HALF, U32) for a in range(2)]
         z_scale = [sb("z_scale_%d" % a, HALF, U8) for a in range(2)]
+
+        def cast_w2(g, engine_copy):
+            dst = w2_bf16[g][:].rearrange("p (c i j) -> p c j i", i=4, j=PACK)
+            src = w2_raw[g][:].rearrange("p j (c i) -> p c j i", i=4)
+            engine_copy(dst, src)
+
+        def quantise_w2(g):
+            nc.vector.quantize_mx(out=w2_codes[g][:].bitcast(FP8X4), scales=w2_scale[g][:], in_=w2_bf16[g][:])
 
         def rectify(q, on_vector):
             dst = z_bf16[q // 2][:, (q % 2) * QUARTER * PACK : (q % 2 + 1) * QUARTER * PACK].rearrange("p (c i t) -> p c t i", i=4, t=PACK)
@@ -172,12 +175,6 @@ def tile_picked_adain8_relu_p_kernel(tc, x_words, x_scales, w1, gamma, beta, w2,
                 nc.vector.tensor_scalar(dst, src, 0.0, None, ALU.max)
             else:
                 nc.scalar.activation(dst, src, ACT.Relu)
-
-        def scale_last(a):
-            nc.vector.tensor_tensor(scaled_last[a], gamma_sb[3][:].indirect(styles(a)), normal[:, half(a)], ALU.mult)
-
-        def shift_last(a):
-            nc.vector.tensor_tensor(pre[:, 3, half(a)], beta_sb[3][:].indirect(styles(a)), scaled_last[a], ALU.add)
 
         def quantise_z(a):
             nc.vector.quantize_mx(out=z_codes[a][:].bitcast(FP8X4), scales=z_scale[a][:], in_=z_bf16[a][:])
@@ -197,35 +194,19 @@ def tile_picked_adain8_relu_p_kernel(tc, x_words, x_scales, w1, gamma, beta, w2,
             engine_copy(staged[:], bank[:])
             nc.sync.dma_start(out[m * P : (m + 1) * P, half(a)], staged[:])
 
-        whole = slice(0, S)
-        centre(0, whole)
-        centre(1, whole)
-        shift(0, whole)
-        shift(1, whole)
-        scale_last(0)
-        scale_last(1)
-        centre(2, half(0))
-        centre(2, half(1))
-        shift(2, half(0))
-        shift_last(0)
-        shift(2, half(1))
-        picked_last = sb("picked_last", HALF, F32)
-        nc.scalar.activation(picked_last[:], beta_sb[3][:].indirect(styles(1)), ACT.Copy)
-        nc.vector.tensor_tensor(pre[:, 3, half(1)], scaled_last[1], picked_last[:], ALU.add)
-        every = slice(0, P // 4)
         rectify(0, False)
         rectify(1, True)
         rectify(2, False)
-        cast_w2(0, every, nc.vector.tensor_copy)
+        cast_w2(0, nc.vector.tensor_copy)
         quantise_z(0)
         quantise_w2(0)
-        cast_w2(1, every, nc.scalar.copy)
-        cast_w2(2, every, nc.scalar.copy)
+        cast_w2(1, nc.scalar.copy)
+        cast_w2(2, nc.scalar.copy)
         rectify(3, True)
         quantise_w2(1)
         quantise_z(1)
         quantise_w2(2)
-        cast_w2(3, every, nc.vector.tensor_copy)
+        cast_w2(3, nc.vector.tensor_copy)
         quantise_w2(3)
         for m, a in ((0, 0), (1, 0), (0, 1), (1, 1)):
             project(m, a, "out_%d" % (2 * a + m), nc.scalar.copy)

@@ -19,8 +19,7 @@ P = 128
 PACK = 4
 HALF = S // 2
 QUARTER = S // 4
-W1_HALF = H // 2
-W1_VECTOR = (42, 42)
+W1_VECTOR = 88
 
 
 def tile_picked_adain8_relu_p_kernel(tc, x_words, x_scales, w1, gamma, beta, w2, offs, sty, out):
@@ -39,7 +38,7 @@ def tile_picked_adain8_relu_p_kernel(tc, x_words, x_scales, w1, gamma, beta, w2,
         sty_sb = keep.tile([P, S // 16], U16, name="sty_sb")
         word_table = sb("word_table", T, U32)
         scale_table = sb("scale_table", T, U8)
-        w1_raw = [keep.tile([P, PACK, W1_HALF], F32, name="w1_raw_%d" % u, align_bytes=64) for u in range(2)]
+        w1_raw = keep.tile([P, PACK, H], F32, name="w1_raw", align_bytes=64)
         w2_raw = [keep.tile([P, PACK, P], F32, name="w2_raw_%d" % g, align_bytes=64) for g in range(PACK)]
         gamma_sb = [sb("gamma_%d" % t, U, F32) for t in range(PACK)]
         beta_sb = [sb("beta_%d" % t, U, F32) for t in range(PACK)]
@@ -57,12 +56,12 @@ def tile_picked_adain8_relu_p_kernel(tc, x_words, x_scales, w1, gamma, beta, w2,
         nc.vector.memset(one, 1.0)
         nc.scalar.activation(eps, one, ACT.Abs_reciprocal_sqrt, scale=1e10)
 
-        nc.sync.dma_start(w1_raw[0][:], w1_rows[:, :, :W1_HALF])
+        nc.sync.dma_start(w1_raw[:, 0:2, :], w1_rows[:, 0:2, :])
         for r in range(4):
             nc.sync.dma_start(scale_table[r:P:32, :].bitcast(I32), x_scales[0, r:16:4, :].bitcast(I32))
         nc.sync.dma_start(offs_sb[:], offs)
+        nc.sync.dma_start(w1_raw[:, 2:4, :], w1_rows[:, 2:4, :])
         nc.sync.dma_start(word_table[:].bitcast(I32), x_words[0].rearrange("p n t -> p (n t)").bitcast(I32))
-        nc.sync.dma_start(w1_raw[1][:], w1_rows[:, :, W1_HALF:])
         nc.sync.dma_start(sty_sb[:], sty)
         for t in range(2):
             nc.sync.dma_start(gamma_sb[t][:], gamma_rows[:, t, :])
@@ -77,36 +76,37 @@ def tile_picked_adain8_relu_p_kernel(tc, x_words, x_scales, w1, gamma, beta, w2,
         x_codes = sb("x_codes", S, U32)
         x_scale = sb("x_scale", S, U8)
         nc.vector.tensor_copy(x_scale[:], scale_table[:].indirect(offs_sb[:]))
-        nc.vector.tensor_copy(x_codes[:], word_table[:].indirect(offs_sb[:]))
 
-        w1_codes = [sb("w1_codes_%d" % t, P, U32) for t in range(PACK)]
-        w1_scale = [sb("w1_scale_%d" % t, P, U8) for t in range(PACK)]
+        w1_bf16 = sb("w1_bf16", H * PACK, BF16)
+        dst = w1_bf16[:].rearrange("p (t m j) -> p m j t", t=PACK, j=PACK)
+        src = w1_raw[:].rearrange("p j (m t) -> p m j t", t=PACK)
+        nc.vector.tensor_copy(dst[:, :W1_VECTOR], src[:, :W1_VECTOR])
+        nc.scalar.copy(dst[:, W1_VECTOR:], src[:, W1_VECTOR:])
+        w1_codes = sb("w1_codes", H, U32)
+        w1_scale = sb("w1_scale", H, U8)
         for u in range(2):
-            w1_bf16 = sb("w1_bf16_%d" % u, W1_HALF * PACK, BF16)
-            dst = w1_bf16[:].rearrange("p (t m j) -> p m j t", t=PACK, j=PACK)
-            src = w1_raw[u][:].rearrange("p j (m t) -> p m j t", t=PACK)
-            nc.scalar.copy(dst[:, W1_VECTOR[u] :], src[:, W1_VECTOR[u] :])
-            nc.vector.tensor_copy(dst[:, : W1_VECTOR[u]], src[:, : W1_VECTOR[u]])
-            cols = slice(u * P // 2, (u + 1) * P // 2)
-            for t in range(PACK):
-                nc.vector.quantize_mx(out=w1_codes[t][:, cols].bitcast(FP8X4), scales=w1_scale[t][:, cols], in_=w1_bf16[:, t * W1_HALF : (t + 1) * W1_HALF])
+            cols = slice(u * H // 2, (u + 1) * H // 2)
+            nc.vector.quantize_mx(out=w1_codes[:, cols].bitcast(FP8X4), scales=w1_scale[:, cols], in_=w1_bf16[:, u * H * PACK // 2 : (u + 1) * H * PACK // 2])
+        for a in range(2):
+            nc.vector.tensor_copy(x_codes[:, half(a)], word_table[:].indirect(offs_sb[:, a * HALF // 16 : (a + 1) * HALF // 16]))
 
         y = [psum.tile([P, S], F32, name="y_%d" % t, tag="y_%d" % t) for t in range(PACK)]
         for t in range(PACK):
-            nc.tensor.matmul_mx(
-                out=y[t][:],
-                lhsT=w1_codes[t][:].bitcast(FP8X4),
-                lhsT_scale=w1_scale[t][:],
-                rhs=x_codes[:].bitcast(FP8X4),
-                rhs_scale=x_scale[:],
-                start=True,
-                stop=True,
-            )
+            for a in range(2):
+                nc.tensor.matmul_mx(
+                    out=y[t][:, half(a)],
+                    lhsT=w1_codes[:, t * P : (t + 1) * P].bitcast(FP8X4),
+                    lhsT_scale=w1_scale[:, t * P : (t + 1) * P],
+                    rhs=x_codes[:, half(a)].bitcast(FP8X4),
+                    rhs_scale=x_scale[:, half(a)],
+                    start=True,
+                    stop=True,
+                )
 
         stats = keep.tile([P, PACK, 8], F32, name="stats")
         for t in range(PACK):
             nc.vector.bn_stats(stats[:, t, 0:6], y[t][:])
-        moments = keep.tile([P, PACK, 2], F32, name="moments", tag="w1_codes_3", align_bytes=64)
+        moments = keep.tile([P, PACK, 2], F32, name="moments", tag="w1_codes", align_bytes=64)
         for t in range(PACK):
             nc.vector.bn_aggr(moments[:, t, :], stats[:, t, 0:6])
 

@@ -37,11 +37,7 @@ def tile_picked_adain8_relu_p_kernel(tc, x_words, x_scales, w1, gamma, beta, w2,
         offs_sb = keep.tile([P, S // 16], U16, name="offs_sb")
         sty_sb = keep.tile([P, S // 16], U16, name="sty_sb")
         word_table = sb("word_table", T, U32)
-        scale_table = sb("scale_table", T, U8)
         w1_raw = keep.tile([P, PACK, H], F32, name="w1_raw", align_bytes=64)
-        w2_raw = [keep.tile([P, PACK, P], F32, name="w2_raw_%d" % g, align_bytes=64) for g in range(PACK)]
-        gamma_sb = [sb("gamma_%d" % t, U, F32) for t in range(PACK)]
-        beta_sb = [sb("beta_%d" % t, U, F32) for t in range(PACK)]
         w1_rows = w1.rearrange("(p j) c -> p j c", j=PACK)
         w2_rows = w2.rearrange("(p j) c -> p j c", j=PACK)
         gamma_rows = gamma.rearrange("(p t) u -> p t u", t=PACK)
@@ -50,19 +46,32 @@ def tile_picked_adain8_relu_p_kernel(tc, x_words, x_scales, w1, gamma, beta, w2,
         def styles(a):
             return sty_sb[:, a * HALF // 16 : (a + 1) * HALF // 16]
 
-        nc.vector.memset(scale_table[:].bitcast(I32), 0)
         consts = keep.tile([P, 2], F32, name="consts")
         one, eps = consts[:, 0:1], consts[:, 1:2]
         nc.vector.memset(one, 1.0)
         nc.scalar.activation(eps, one, ACT.Abs_reciprocal_sqrt, scale=1e10)
 
-        nc.sync.dma_start(w1_raw[:, 0:2, :], w1_rows[:, 0:2, :])
+        x_codes = sb("x_codes", S, U32)
+        picked_scale = sb("picked_scale", S, U8)
+        x_scale = sb("x_scale", S, U8)
+        with tc.tile_pool(name="early", bufs=1) as early:
+            scale_table = early.tile([P, T], U8, name="scale_table", align_bytes=64)
+            nc.vector.memset(scale_table[:].bitcast(I32), 0)
+            nc.vector.memset(x_scale[:].bitcast(I32), 0)
+            nc.sync.dma_start(w1_raw[:, 0:1, :], w1_rows[:, 0:1, :])
+            nc.sync.dma_start(scale_table[0:P:8, :].bitcast(I32), x_scales[0].bitcast(I32))
+            nc.sync.dma_start(offs_sb[:], offs)
+            nc.sync.dma_start(sty_sb[:], sty)
+            nc.sync.dma_start(w1_raw[:, 1:4, :], w1_rows[:, 1:4, :])
+            nc.sync.dma_start(word_table[:].bitcast(I32), x_words[0].rearrange("p n t -> p (n t)").bitcast(I32))
+            nc.vector.tensor_copy(picked_scale[:], scale_table[:].indirect(offs_sb[:]))
         for r in range(4):
-            nc.sync.dma_start(scale_table[r:P:32, :].bitcast(I32), x_scales[0, r:16:4, :].bitcast(I32))
-        nc.sync.dma_start(offs_sb[:], offs)
-        nc.sync.dma_start(w1_raw[:, 2:4, :], w1_rows[:, 2:4, :])
-        nc.sync.dma_start(word_table[:].bitcast(I32), x_words[0].rearrange("p n t -> p (n t)").bitcast(I32))
-        nc.sync.dma_start(sty_sb[:], sty)
+            nc.sync.dma_start(x_scale[r:P:32, :].bitcast(I32), picked_scale[8 * r : P : 32, :].bitcast(I32))
+
+        late = ctx.enter_context(tc.tile_pool(name="late", bufs=1))
+        gamma_sb = [late.tile([P, U], F32, name="gamma_%d" % t, tag="gamma_%d" % t, align_bytes=64) for t in range(PACK)]
+        beta_sb = [late.tile([P, U], F32, name="beta_%d" % t, align_bytes=64) for t in range(PACK)]
+        w2_raw = [late.tile([P, PACK, P], F32, name="w2_raw_%d" % g, align_bytes=64) for g in range(PACK)]
         for t in range(2):
             nc.sync.dma_start(gamma_sb[t][:], gamma_rows[:, t, :])
             nc.sync.dma_start(beta_sb[t][:], beta_rows[:, t, :])
@@ -72,10 +81,6 @@ def tile_picked_adain8_relu_p_kernel(tc, x_words, x_scales, w1, gamma, beta, w2,
             nc.sync.dma_start(beta_sb[t][:], beta_rows[:, t, :])
         for g in range(PACK):
             nc.sync.dma_start(w2_raw[g][:], w2_rows[:, :, g * P : (g + 1) * P])
-
-        x_codes = sb("x_codes", S, U32)
-        x_scale = sb("x_scale", S, U8)
-        nc.vector.tensor_copy(x_scale[:], scale_table[:].indirect(offs_sb[:]))
 
         w1_bf16 = sb("w1_bf16", H * PACK, BF16)
         dst = w1_bf16[:].rearrange("p (t m j) -> p m j t", t=PACK, j=PACK)
@@ -90,11 +95,11 @@ def tile_picked_adain8_relu_p_kernel(tc, x_words, x_scales, w1, gamma, beta, w2,
         for a in range(2):
             nc.vector.tensor_copy(x_codes[:, half(a)], word_table[:].indirect(offs_sb[:, a * HALF // 16 : (a + 1) * HALF // 16]))
 
-        y = [psum.tile([P, S], F32, name="y_%d" % t, tag="y_%d" % t) for t in range(PACK)]
-        for t in range(PACK):
-            for a in range(2):
+        y = [[psum.tile([P, HALF], F32, name="y_%d_%d" % (t, a), tag="bank_%d" % (2 * t + a)) for a in range(2)] for t in range(PACK)]
+        for a in range(2):
+            for t in range(PACK):
                 nc.tensor.matmul_mx(
-                    out=y[t][:, half(a)],
+                    out=y[t][a][:],
                     lhsT=w1_codes[:, t * P : (t + 1) * P].bitcast(FP8X4),
                     lhsT_scale=w1_scale[:, t * P : (t + 1) * P],
                     rhs=x_codes[:, half(a)].bitcast(FP8X4),
@@ -103,12 +108,13 @@ def tile_picked_adain8_relu_p_kernel(tc, x_words, x_scales, w1, gamma, beta, w2,
                     stop=True,
                 )
 
-        stats = keep.tile([P, PACK, 8], F32, name="stats")
-        for t in range(PACK):
-            nc.vector.bn_stats(stats[:, t, 0:6], y[t][:])
+        stats = keep.tile([P, PACK, 12], F32, name="stats")
+        for a in range(2):
+            for t in range(PACK):
+                nc.vector.bn_stats(stats[:, t, 6 * a : 6 * a + 6], y[t][a][:])
         moments = keep.tile([P, PACK, 2], F32, name="moments", tag="w1_codes", align_bytes=64)
         for t in range(PACK):
-            nc.vector.bn_aggr(moments[:, t, :], stats[:, t, 0:6])
+            nc.vector.bn_aggr(moments[:, t, :], stats[:, t, :])
 
         picked_gamma = [sb("picked_gamma_%d" % t, S, F32) for t in range(3)]
         picked_beta = [sb("picked_beta_%d" % t, S, F32) for t in range(3)]
@@ -120,24 +126,26 @@ def tile_picked_adain8_relu_p_kernel(tc, x_words, x_scales, w1, gamma, beta, w2,
         pick(picked_gamma[0][:], gamma_sb[0], sty_sb[:])
         pick(picked_beta[0][:], beta_sb[0], sty_sb[:])
         pick(picked_gamma[1][:], gamma_sb[1], sty_sb[:])
-        rstd = sb("rstd", PACK, F32, tag="gamma_1")
+        rstd = late.tile([P, PACK], F32, name="rstd", tag="gamma_1", align_bytes=64)
         nc.scalar.activation(rstd[:], moments[:, :, 1], ACT.Abs_reciprocal_sqrt, bias=eps)
         pick(picked_beta[1][:], beta_sb[1], sty_sb[:])
         normal = sb("normal", S, F32)
         scaled = [sb("scaled_0", S, F32), sb("scaled_1", S, F32), normal, sb("scaled_3", S, F32)]
         pre = keep.tile([P, PACK, S], F32, name="pre", align_bytes=64)
 
-        def centre(t, places):
-            nc.vector.scalar_tensor_tensor(scaled[t][:, places], y[t][:, places], moments[:, t, 0:1], picked_gamma[t][:, places], ALU.subtract, ALU.mult)
+        def centre(t, a):
+            nc.vector.scalar_tensor_tensor(scaled[t][:, half(a)], y[t][a][:], moments[:, t, 0:1], picked_gamma[t][:, half(a)], ALU.subtract, ALU.mult)
 
         def shift(t, places):
             nc.vector.scalar_tensor_tensor(pre[:, t, places], scaled[t][:, places], rstd[:, t : t + 1], picked_beta[t][:, places], ALU.mult, ALU.add)
 
         whole = slice(0, S)
-        centre(0, whole)
-        centre(1, whole)
+        for t in range(2):
+            for a in range(2):
+                centre(t, a)
         shift(0, whole)
-        nc.vector.tensor_scalar(normal[:], y[3][:], moments[:, 3, 0:1], rstd[:, 3:4], ALU.subtract, ALU.mult)
+        for a in range(2):
+            nc.vector.tensor_scalar(normal[:, half(a)], y[3][a][:], moments[:, 3, 0:1], rstd[:, 3:4], ALU.subtract, ALU.mult)
         shift(1, whole)
 
         pick(picked_gamma[2][:], gamma_sb[2], sty_sb[:])
@@ -145,8 +153,8 @@ def tile_picked_adain8_relu_p_kernel(tc, x_words, x_scales, w1, gamma, beta, w2,
             pick(picked_beta[2][:, half(a)], beta_sb[2], styles(a))
         for a in range(2):
             nc.vector.tensor_tensor(scaled[3][:, half(a)], gamma_sb[3][:].indirect(styles(a)), normal[:, half(a)], ALU.mult)
-        centre(2, half(0))
-        centre(2, half(1))
+        centre(2, 0)
+        centre(2, 1)
         shift(2, half(0))
         shift(2, half(1))
         pick(late_beta[:], beta_sb[3], styles(1))
@@ -209,6 +217,6 @@ def tile_picked_adain8_relu_p_kernel(tc, x_words, x_scales, w1, gamma, beta, w2,
         cast_w2(3, nc.vector.tensor_copy)
         quantise_w2(3)
         for m, a in ((0, 0), (1, 0), (0, 1), (1, 1)):
-            project(m, a, "out_%d" % (2 * a + m), nc.scalar.copy)
+            project(m, a, "bank_%d" % (2 * a + m), nc.scalar.copy)
         for m, a in ((2, 0), (2, 1), (3, 0), (3, 1)):
-            project(m, a, "y_%d" % (2 * (m - 2) + a), nc.vector.tensor_copy if a == 0 else nc.scalar.copy)
+            project(m, a, "bank_%d" % (2 * m + a), nc.vector.tensor_copy if a == 0 else nc.scalar.copy)

@@ -70,7 +70,7 @@ def tile_picked_adain8_relu_p_kernel(tc, x_words, x_scales, w1, gamma, beta, w2,
 
         late = ctx.enter_context(tc.tile_pool(name="late", bufs=1))
         gamma_sb = [late.tile([P, U], F32, name="gamma_%d" % t, tag="gamma_%d" % t, align_bytes=64) for t in range(PACK)]
-        beta_sb = [late.tile([P, U], F32, name="beta_%d" % t, align_bytes=64) for t in range(PACK)]
+        beta_sb = [late.tile([P, U], F32, name="beta_%d" % t, tag="beta_%d" % t, align_bytes=64) for t in range(PACK)]
         w2_raw = [late.tile([P, PACK, P], F32, name="w2_raw_%d" % g, align_bytes=64) for g in range(PACK)]
         for t in range(2):
             nc.sync.dma_start(gamma_sb[t][:], gamma_rows[:, t, :])
@@ -118,7 +118,6 @@ def tile_picked_adain8_relu_p_kernel(tc, x_words, x_scales, w1, gamma, beta, w2,
 
         picked_gamma = [sb("picked_gamma_%d" % t, S, F32) for t in range(3)]
         picked_beta = [sb("picked_beta_%d" % t, S, F32) for t in range(3)]
-        late_beta = sb("late_beta", HALF, F32)
 
         def pick(dst, table, offsets):
             nc.scalar.activation(dst, table[:].indirect(offsets), ACT.Copy)
@@ -156,15 +155,15 @@ def tile_picked_adain8_relu_p_kernel(tc, x_words, x_scales, w1, gamma, beta, w2,
         centre(2, 0)
         centre(2, 1)
         shift(2, half(0))
-        shift(2, half(1))
-        pick(late_beta[:], beta_sb[3], styles(1))
+        late_beta = pre[:, 2, half(1)]
+        pick(late_beta, beta_sb[3], styles(1))
         nc.vector.tensor_tensor(pre[:, 3, half(0)], beta_sb[3][:].indirect(styles(0)), scaled[3][:, half(0)], ALU.add)
-        nc.vector.tensor_tensor(pre[:, 3, half(1)], late_beta[:], scaled[3][:, half(1)], ALU.add)
+        nc.vector.tensor_tensor(pre[:, 3, half(1)], late_beta, scaled[3][:, half(1)], ALU.add)
 
         w2_bf16 = [sb("w2_bf16_%d" % g, P * PACK, BF16) for g in range(PACK)]
         w2_codes = [sb("w2_codes_%d" % g, P, U32) for g in range(PACK)]
         w2_scale = [sb("w2_scale_%d" % g, P, U8) for g in range(PACK)]
-        z_bf16 = [sb("z_bf16_%d" % a, HALF * PACK, BF16) for a in range(2)]
+        z_bf16 = [late.tile([P, HALF * PACK], BF16, name="z_bf16_0", tag="beta_3", align_bytes=64), sb("z_bf16_1", HALF * PACK, BF16)]
         z_codes = [sb("z_codes_%d" % a, HALF, U32) for a in range(2)]
         z_scale = [sb("z_scale_%d" % a, HALF, U8) for a in range(2)]
 
@@ -204,11 +203,12 @@ def tile_picked_adain8_relu_p_kernel(tc, x_words, x_scales, w1, gamma, beta, w2,
 
         rectify(0, False)
         rectify(1, True)
-        rectify(2, False)
+        shift(2, half(1))
         cast_w2(0, nc.vector.tensor_copy)
         quantise_z(0)
         quantise_w2(0)
         cast_w2(1, nc.scalar.copy)
+        rectify(2, False)
         cast_w2(2, nc.scalar.copy)
         rectify(3, True)
         quantise_w2(1)

@@ -112,7 +112,7 @@ def tile_picked_adain8_relu_p_kernel(tc, x_words, x_scales, w1, gamma, beta, w2,
         for a in range(2):
             for t in range(PACK):
                 nc.vector.bn_stats(stats[:, t, 6 * a : 6 * a + 6], y[t][a][:])
-        moments = keep.tile([P, PACK, 2], F32, name="moments", tag="w1_codes", align_bytes=64)
+        moments = keep.tile([P, PACK, 2], F32, name="moments", tag="x_scale", align_bytes=64)
         for t in range(PACK):
             nc.vector.bn_aggr(moments[:, t, :], stats[:, t, :])
 
@@ -154,6 +154,17 @@ def tile_picked_adain8_relu_p_kernel(tc, x_words, x_scales, w1, gamma, beta, w2,
             nc.vector.tensor_tensor(scaled[3][:, half(a)], gamma_sb[3][:].indirect(styles(a)), normal[:, half(a)], ALU.mult)
         centre(2, 0)
         centre(2, 1)
+        warm = psum.tile([P, S], F32, name="warm", tag="bank_5")
+        for k in range(3):
+            nc.tensor.matmul_mx(
+                out=warm[:32, :],
+                lhsT=w1_codes[:, 64 * k : 64 * k + 32].bitcast(FP8X4),
+                lhsT_scale=w1_scale[:, 64 * k : 64 * k + 32],
+                rhs=w1_codes[:].bitcast(FP8X4),
+                rhs_scale=w1_scale[:],
+                start=True,
+                stop=True,
+            )
         shift(2, half(0))
         late_beta = pre[:, 2, half(1)]
         pick(late_beta, beta_sb[3], styles(1))

@@ -61,9 +61,9 @@ def tile_picked_adain8_relu_p_kernel(tc, x_words, x_scales, w1, gamma, beta, w2,
             nc.sync.dma_start(w1_raw[:, 0:1, :], w1_rows[:, 0:1, :])
             nc.sync.dma_start(scale_table[0:P:8, :].bitcast(I32), x_scales[0].bitcast(I32))
             nc.sync.dma_start(offs_sb[:], offs)
-            nc.sync.dma_start(sty_sb[:], sty)
             nc.sync.dma_start(w1_raw[:, 1:4, :], w1_rows[:, 1:4, :])
             nc.sync.dma_start(word_table[:].bitcast(I32), x_words[0].rearrange("p n t -> p (n t)").bitcast(I32))
+            nc.sync.dma_start(sty_sb[:], sty)
             nc.vector.tensor_copy(picked_scale[:], scale_table[:].indirect(offs_sb[:]))
         for r in range(4):
             nc.sync.dma_start(x_scale[r:P:32, :].bitcast(I32), picked_scale[8 * r : P : 32, :].bitcast(I32))
@@ -142,9 +142,11 @@ def tile_picked_adain8_relu_p_kernel(tc, x_words, x_scales, w1, gamma, beta, w2,
         for t in range(2):
             for a in range(2):
                 centre(t, a)
+        offset = keep.tile([P, 1], F32, name="offset")
+        nc.vector.tensor_scalar(offset[:], moments[:, 3, 0:1], rstd[:, 3:4], -1.0, ALU.mult, ALU.mult)
+        nc.scalar.activation(normal[:, half(1)], y[3][1][:], ACT.Identity, scale=rstd[:, 3:4], bias=offset[:])
         shift(0, whole)
-        for a in range(2):
-            nc.vector.tensor_scalar(normal[:, half(a)], y[3][a][:], moments[:, 3, 0:1], rstd[:, 3:4], ALU.subtract, ALU.mult)
+        nc.vector.tensor_scalar(normal[:, half(0)], y[3][0][:], moments[:, 3, 0:1], rstd[:, 3:4], ALU.subtract, ALU.mult)
         shift(1, whole)
 
         pick(picked_gamma[2][:], gamma_sb[2], sty_sb[:])
@@ -230,4 +232,4 @@ def tile_picked_adain8_relu_p_kernel(tc, x_words, x_scales, w1, gamma, beta, w2,
         for m, a in ((0, 0), (1, 0), (0, 1), (1, 1)):
             project(m, a, "bank_%d" % (2 * a + m), nc.scalar.copy)
         for m, a in ((2, 0), (2, 1), (3, 0), (3, 1)):
-            project(m, a, "bank_%d" % (2 * m + a), nc.vector.tensor_copy if a == 0 else nc.scalar.copy)
+            project(m, a, "bank_%d" % (2 * m + a), nc.scalar.copy if (m, a) == (2, 1) else nc.vector.tensor_copy)

@@ -232,4 +232,4 @@ def tile_picked_adain8_relu_p_kernel(tc, x_words, x_scales, w1, gamma, beta, w2,
         for m, a in ((0, 0), (1, 0), (0, 1), (1, 1)):
             project(m, a, "bank_%d" % (2 * a + m), nc.scalar.copy)
         for m, a in ((2, 0), (2, 1), (3, 0), (3, 1)):
-            project(m, a, "bank_%d" % (2 * m + a), nc.scalar.copy if (m, a) == (2, 1) else nc.vector.tensor_copy)
+            project(m, a, "bank_%d" % (2 * m + a), nc.scalar.copy if m == 2 else nc.vector.tensor_copy)

@@ -196,10 +196,14 @@ def tile_picked_adain8_relu_p_kernel(tc, x_words, x_scales, w1, gamma, beta, w2,
             else:
                 nc.scalar.activation(dst, src, ACT.Relu)
 
-        def quantise_z(a):
-            nc.vector.quantize_mx(out=z_codes[a][:].bitcast(FP8X4), scales=z_scale[a][:], in_=z_bf16[a][:])
+        def quantise_z(a, first, width):
+            nc.vector.quantize_mx(
+                out=z_codes[a][:, first : first + width].bitcast(FP8X4),
+                scales=z_scale[a][:, first : first + width],
+                in_=z_bf16[a][:, first * PACK : (first + width) * PACK],
+            )
 
-        def project(m, a, tag, engine_copy):
+        def project(m, a, tag, engine_copy, staged):
             bank = psum.tile([P, HALF], F32, name="o_%d_%d" % (m, a), tag=tag)
             nc.tensor.matmul_mx(
                 out=bank[:],
@@ -210,26 +214,51 @@ def tile_picked_adain8_relu_p_kernel(tc, x_words, x_scales, w1, gamma, beta, w2,
                 start=True,
                 stop=True,
             )
+            engine_copy(staged, bank[:])
+
+        def project_and_store(m, a, tag):
             staged = sb("staged_%d_%d" % (m, a), HALF, F32)
-            engine_copy(staged[:], bank[:])
+            project(m, a, tag, nc.scalar.copy, staged[:])
             nc.sync.dma_start(out[m * P : (m + 1) * P, half(a)], staged[:])
 
         rectify(0, False)
         rectify(1, True)
         shift(2, half(1))
         cast_w2(0, nc.vector.tensor_copy)
-        quantise_z(0)
+        quantise_z(0, 0, HALF)
         quantise_w2(0)
         cast_w2(1, nc.scalar.copy)
         rectify(2, False)
         cast_w2(2, nc.scalar.copy)
         rectify(3, True)
         quantise_w2(1)
-        quantise_z(1)
+        quantise_z(1, QUARTER, QUARTER)
+        quantise_z(1, 0, QUARTER)
         quantise_w2(2)
         cast_w2(3, nc.vector.tensor_copy)
         quantise_w2(3)
-        for m, a in ((0, 0), (1, 0), (0, 1), (1, 1)):
-            project(m, a, "bank_%d" % (2 * a + m), nc.scalar.copy)
-        for m, a in ((2, 0), (2, 1), (3, 0), (3, 1)):
-            project(m, a, "bank_%d" % (2 * m + a), nc.scalar.copy if m == 2 else nc.vector.tensor_copy)
+        for m in range(2):
+            project_and_store(m, 0, "bank_%d" % m)
+        upper_rows = out[: 2 * P, :].rearrange("(m p) c -> p m c", p=P)
+        for q in (1, 0):
+            places = slice(q * QUARTER, (q + 1) * QUARTER)
+            bank = psum.tile([P, 2, QUARTER], F32, name="o_quarter_%d" % q, tag="bank_%d" % (2 + q))
+            for m in range(2):
+                nc.tensor.matmul_mx(
+                    out=bank[:, m, :],
+                    lhsT=w2_codes[m][:].bitcast(FP8X4),
+                    lhsT_scale=w2_scale[m][:],
+                    rhs=z_codes[1][:, places].bitcast(FP8X4),
+                    rhs_scale=z_scale[1][:, places],
+                    start=True,
+                    stop=True,
+                )
+            staged = keep.tile([P, 2, QUARTER], F32, name="staged_quarter_%d" % q, align_bytes=64)
+            nc.scalar.copy(staged[:], bank[:])
+            nc.sync.dma_start(upper_rows[:, :, HALF + q * QUARTER : HALF + (q + 1) * QUARTER], staged[:])
+        for a in range(2):
+            project_and_store(2, a, "bank_%d" % (4 + a))
+        last_rows = sb("last_rows", S, F32)
+        for a in range(2):
+            project(3, a, "bank_%d" % (6 + a), nc.vector.tensor_copy, last_rows[:, half(a)])
+        nc.sync.dma_start(out[3 * P :, :], last_rows[:])

from contextlib import ExitStack

import concourse.mybir as mybir

K, T, S, N, H, U = 512, 2048, 512, 512, 512, 1024
FLOPS = 2 * K * H * S + 2 * H * N * S

F32 = mybir.dt.float32
BF16 = mybir.dt.bfloat16
I32 = mybir.dt.int32
U32 = mybir.dt.uint32
U16 = mybir.dt.uint16
U8 = mybir.dt.uint8
FP8X4 = mybir.dt.float8_e4m3fn_x4
ACT = mybir.ActivationFunctionType
ALU = mybir.AluOpType

P = 128
PACK = 4
HALF = S // 2
QUARTER = S // 4
W1_VECTOR = 88


def tile_picked_adain8_relu_p_kernel(tc, x_words, x_scales, w1, gamma, beta, w2, offs, sty, out):
    nc = tc.nc
    with ExitStack() as ctx:
        keep = ctx.enter_context(tc.tile_pool(name="keep", bufs=1))
        psum = ctx.enter_context(tc.psum_pool(name="psum", bufs=1))

        def sb(name, cols, dtype, tag=None):
            return keep.tile([P, cols], dtype, name=name, tag=tag or name, align_bytes=64)

        def half(a):
            return slice(a * HALF, (a + 1) * HALF)

        offs_sb = keep.tile([P, S // 16], U16, name="offs_sb")
        sty_sb = keep.tile([P, S // 16], U16, name="sty_sb")
        word_table = sb("word_table", T, U32)
        w1_raw = keep.tile([P, PACK, H], F32, name="w1_raw", align_bytes=64)
        w1_rows = w1.rearrange("(p j) c -> p j c", j=PACK)
        w2_rows = w2.rearrange("(p j) c -> p j c", j=PACK)
        gamma_rows = gamma.rearrange("(p t) u -> p t u", t=PACK)
        beta_rows = beta.rearrange("(p t) u -> p t u", t=PACK)

        def styles(a):
            return sty_sb[:, a * HALF // 16 : (a + 1) * HALF // 16]

        consts = keep.tile([P, 2], F32, name="consts")
        one, eps = consts[:, 0:1], consts[:, 1:2]
        nc.vector.memset(one, 1.0)
        nc.scalar.activation(eps, one, ACT.Abs_reciprocal_sqrt, scale=1e10)

        x_codes = sb("x_codes", S, U32)
        picked_scale = sb("picked_scale", S, U8)
        x_scale = sb("x_scale", S, U8)
        with tc.tile_pool(name="early", bufs=1) as early:
            scale_table = early.tile([P, T], U8, name="scale_table", align_bytes=64)
            nc.vector.memset(scale_table[:].bitcast(I32), 0)
            nc.vector.memset(x_scale[:].bitcast(I32), 0)
            nc.sync.dma_start(w1_raw[:, 0:1, :], w1_rows[:, 0:1, :])
            nc.sync.dma_start(scale_table[0:P:8, :].bitcast(I32), x_scales[0].bitcast(I32))
            nc.sync.dma_start(offs_sb[:], offs)
            nc.sync.dma_start(w1_raw[:, 1:4, :], w1_rows[:, 1:4, :])
            nc.sync.dma_start(word_table[:].bitcast(I32), x_words[0].rearrange("p n t -> p (n t)").bitcast(I32))
            nc.sync.dma_start(sty_sb[:], sty)
            nc.vector.tensor_copy(picked_scale[:], scale_table[:].indirect(offs_sb[:]))
        for r in range(4):
            nc.sync.dma_start(x_scale[r:P:32, :].bitcast(I32), picked_scale[8 * r : P : 32, :].bitcast(I32))

        late = ctx.enter_context(tc.tile_pool(name="late", bufs=1))
        gamma_sb = [late.tile([P, U], F32, name="gamma_%d" % t, tag="gamma_%d" % t, align_bytes=64) for t in range(PACK)]
        beta_sb = [late.tile([P, U], F32, name="beta_%d" % t, tag="beta_%d" % t, align_bytes=64) for t in range(PACK)]
        w2_raw = [late.tile([P, PACK, P], F32, name="w2_raw_%d" % g, align_bytes=64) for g in range(PACK)]
        for t in range(2):
            nc.sync.dma_start(gamma_sb[t][:], gamma_rows[:, t, :])
            nc.sync.dma_start(beta_sb[t][:], beta_rows[:, t, :])
        for t in (2, 3):
            nc.sync.dma_start(gamma_sb[t][:], gamma_rows[:, t, :])
        for t in (2, 3):
            nc.sync.dma_start(beta_sb[t][:], beta_rows[:, t, :])
        for g in range(PACK):
            nc.sync.dma_start(w2_raw[g][:], w2_rows[:, :, g * P : (g + 1) * P])

        w1_bf16 = sb("w1_bf16", H * PACK, BF16)
        dst = w1_bf16[:].rearrange("p (t m j) -> p m j t", t=PACK, j=PACK)
        src = w1_raw[:].rearrange("p j (m t) -> p m j t", t=PACK)
        nc.vector.tensor_copy(dst[:, :W1_VECTOR], src[:, :W1_VECTOR])
        nc.scalar.copy(dst[:, W1_VECTOR:], src[:, W1_VECTOR:])
        w1_codes = sb("w1_codes", H, U32)
        w1_scale = sb("w1_scale", H, U8)
        for u in range(2):
            cols = slice(u * H // 2, (u + 1) * H // 2)
            nc.vector.quantize_mx(out=w1_codes[:, cols].bitcast(FP8X4), scales=w1_scale[:, cols], in_=w1_bf16[:, u * H * PACK // 2 : (u + 1) * H * PACK // 2])
        for a in range(2):
            nc.vector.tensor_copy(x_codes[:, half(a)], word_table[:].indirect(offs_sb[:, a * HALF // 16 : (a + 1) * HALF // 16]))

        y = [[psum.tile([P, HALF], F32, name="y_%d_%d" % (t, a), tag="bank_%d" % (2 * t + a)) for a in range(2)] for t in range(PACK)]
        for a in range(2):
            for t in range(PACK):
                nc.tensor.matmul_mx(
                    out=y[t][a][:],
                    lhsT=w1_codes[:, t * P : (t + 1) * P].bitcast(FP8X4),
                    lhsT_scale=w1_scale[:, t * P : (t + 1) * P],
                    rhs=x_codes[:, half(a)].bitcast(FP8X4),
                    rhs_scale=x_scale[:, half(a)],
                    start=True,
                    stop=True,
                )

        stats = keep.tile([P, PACK, 12], F32, name="stats")
        for a in range(2):
            for t in range(PACK):
                nc.vector.bn_stats(stats[:, t, 6 * a : 6 * a + 6], y[t][a][:])
        moments = keep.tile([P, PACK, 2], F32, name="moments", tag="x_scale", align_bytes=64)
        for t in range(PACK):
            nc.vector.bn_aggr(moments[:, t, :], stats[:, t, :])

        picked_gamma = [sb("picked_gamma_%d" % t, S, F32) for t in range(3)]
        picked_beta = [sb("picked_beta_%d" % t, S, F32) for t in range(3)]

        def pick(dst, table, offsets):
            nc.scalar.activation(dst, table[:].indirect(offsets), ACT.Copy)

        pick(picked_gamma[0][:], gamma_sb[0], sty_sb[:])
        pick(picked_beta[0][:], beta_sb[0], sty_sb[:])
        pick(picked_gamma[1][:], gamma_sb[1], sty_sb[:])
        rstd = late.tile([P, PACK], F32, name="rstd", tag="gamma_1", align_bytes=64)
        nc.scalar.activation(rstd[:], moments[:, :, 1], ACT.Abs_reciprocal_sqrt, bias=eps)
        pick(picked_beta[1][:], beta_sb[1], sty_sb[:])
        normal = sb("normal", S, F32)
        scaled = [sb("scaled_0", S, F32), sb("scaled_1", S, F32), normal, sb("scaled_3", S, F32)]
        pre = keep.tile([P, PACK, S], F32, name="pre", align_bytes=64)

        def centre(t, a):
            nc.vector.scalar_tensor_tensor(scaled[t][:, half(a)], y[t][a][:], moments[:, t, 0:1], picked_gamma[t][:, half(a)], ALU.subtract, ALU.mult)

        def shift(t, places):
            nc.vector.scalar_tensor_tensor(pre[:, t, places], scaled[t][:, places], rstd[:, t : t + 1], picked_beta[t][:, places], ALU.mult, ALU.add)

        whole = slice(0, S)
        for t in range(2):
            for a in range(2):
                centre(t, a)
        offset = keep.tile([P, 1], F32, name="offset")
        nc.vector.tensor_scalar(offset[:], moments[:, 3, 0:1], rstd[:, 3:4], -1.0, ALU.mult, ALU.mult)
        nc.scalar.activation(normal[:, half(1)], y[3][1][:], ACT.Identity, scale=rstd[:, 3:4], bias=offset[:])
        shift(0, whole)
        nc.vector.tensor_scalar(normal[:, half(0)], y[3][0][:], moments[:, 3, 0:1], rstd[:, 3:4], ALU.subtract, ALU.mult)
        shift(1, whole)

        pick(picked_gamma[2][:], gamma_sb[2], sty_sb[:])
        for a in range(2):
            pick(picked_beta[2][:, half(a)], beta_sb[2], styles(a))
        for a in range(2):
            nc.vector.tensor_tensor(scaled[3][:, half(a)], gamma_sb[3][:].indirect(styles(a)), normal[:, half(a)], ALU.mult)
        centre(2, 0)
        centre(2, 1)
        warm = psum.tile([P, S], F32, name="warm", tag="bank_5")
        for k in range(3):
            nc.tensor.matmul_mx(
                out=warm[:32, :],
                lhsT=w1_codes[:, 64 * k : 64 * k + 32].bitcast(FP8X4),
                lhsT_scale=w1_scale[:, 64 * k : 64 * k + 32],
                rhs=w1_codes[:].bitcast(FP8X4),
                rhs_scale=w1_scale[:],
                start=True,
                stop=True,
            )
        shift(2, half(0))
        late_beta = pre[:, 2, half(1)]
        pick(late_beta, beta_sb[3], styles(1))
        nc.vector.tensor_tensor(pre[:, 3, half(0)], beta_sb[3][:].indirect(styles(0)), scaled[3][:, half(0)], ALU.add)
        nc.vector.tensor_tensor(pre[:, 3, half(1)], late_beta, scaled[3][:, half(1)], ALU.add)

        w2_bf16 = [sb("w2_bf16_%d" % g, P * PACK, BF16) for g in range(PACK)]
        w2_codes = [sb("w2_codes_%d" % g, P, U32) for g in range(PACK)]
        w2_scale = [sb("w2_scale_%d" % g, P, U8) for g in range(PACK)]
        z_bf16 = [late.tile([P, HALF * PACK], BF16, name="z_bf16_0", tag="beta_3", align_bytes=64), sb("z_bf16_1", HALF * PACK, BF16)]
        z_codes = [sb("z_codes_%d" % a, HALF, U32) for a in range(2)]
        z_scale = [sb("z_scale_%d" % a, HALF, U8) for a in range(2)]

        def cast_w2(g, engine_copy):
            dst = w2_bf16[g][:].rearrange("p (c i j) -> p c j i", i=4, j=PACK)
            src = w2_raw[g][:].rearrange("p j (c i) -> p c j i", i=4)
            engine_copy(dst, src)

        def quantise_w2(g):
            nc.vector.quantize_mx(out=w2_codes[g][:].bitcast(FP8X4), scales=w2_scale[g][:], in_=w2_bf16[g][:])

        def rectify(q, on_vector):
            dst = z_bf16[q // 2][:, (q % 2) * QUARTER * PACK : (q % 2 + 1) * QUARTER * PACK].rearrange("p (c i t) -> p c t i", i=4, t=PACK)
            src = pre[:, :, q * QUARTER : (q + 1) * QUARTER].rearrange("p t (c i) -> p c t i", i=4)
            if on_vector:
                nc.vector.tensor_scalar(dst, src, 0.0, None, ALU.max)
            else:
                nc.scalar.activation(dst, src, ACT.Relu)

        def quantise_z(a, first, width):
            nc.vector.quantize_mx(
                out=z_codes[a][:, first : first + width].bitcast(FP8X4),
                scales=z_scale[a][:, first : first + width],
                in_=z_bf16[a][:, first * PACK : (first + width) * PACK],
            )

        def project(m, a, tag, engine_copy, staged):
            bank = psum.tile([P, HALF], F32, name="o_%d_%d" % (m, a), tag=tag)
            nc.tensor.matmul_mx(
                out=bank[:],
                lhsT=w2_codes[m][:].bitcast(FP8X4),
                lhsT_scale=w2_scale[m][:],
                rhs=z_codes[a][:].bitcast(FP8X4),
                rhs_scale=z_scale[a][:],
                start=True,
                stop=True,
            )
            engine_copy(staged, bank[:])

        def project_and_store(m, a, tag):
            staged = sb("staged_%d_%d" % (m, a), HALF, F32)
            project(m, a, tag, nc.scalar.copy, staged[:])
            nc.sync.dma_start(out[m * P : (m + 1) * P, half(a)], staged[:])

        rectify(0, False)
        rectify(1, True)
        shift(2, half(1))
        cast_w2(0, nc.vector.tensor_copy)
        quantise_z(0, 0, HALF)
        quantise_w2(0)
        cast_w2(1, nc.scalar.copy)
        rectify(2, False)
        cast_w2(2, nc.scalar.copy)
        rectify(3, True)
        quantise_w2(1)
        quantise_z(1, QUARTER, QUARTER)
        quantise_z(1, 0, QUARTER)
        quantise_w2(2)
        cast_w2(3, nc.vector.tensor_copy)
        quantise_w2(3)
        for m in range(2):
            project_and_store(m, 0, "bank_%d" % m)
        upper_rows = out[: 2 * P, :].rearrange("(m p) c -> p m c", p=P)
        for q in (1, 0):
            places = slice(q * QUARTER, (q + 1) * QUARTER)
            bank = psum.tile([P, 2, QUARTER], F32, name="o_quarter_%d" % q, tag="bank_%d" % (2 + q))
            for m in range(2):
                nc.tensor.matmul_mx(
                    out=bank[:, m, :],
                    lhsT=w2_codes[m][:].bitcast(FP8X4),
                    lhsT_scale=w2_scale[m][:],
                    rhs=z_codes[1][:, places].bitcast(FP8X4),
                    rhs_scale=z_scale[1][:, places],
                    start=True,
                    stop=True,
                )
            staged = keep.tile([P, 2, QUARTER], F32, name="staged_quarter_%d" % q, align_bytes=64)
            nc.scalar.copy(staged[:], bank[:])
            nc.sync.dma_start(upper_rows[:, :, HALF + q * QUARTER : HALF + (q + 1) * QUARTER], staged[:])
        for a in range(2):
            project_and_store(2, a, "bank_%d" % (4 + a))
        last_rows = sb("last_rows", S, F32)
        for a in range(2):
            project(3, a, "bank_%d" % (6 + a), nc.vector.tensor_copy, last_rows[:, half(a)])
        nc.sync.dma_start(out[3 * P :, :], last_rows[:])
